import numpy as np, ml_dtypes
CORES = [1,5,17,21,33,37,49,53]
N = 8
import mx_ref
BF = ml_dtypes.bfloat16
def gentries(a):
    return np.ascontiguousarray(a.reshape(8, 16, -1).transpose(0, 2, 1)).reshape(8, -1)
def gtable(e):
    e = np.asarray(e); return np.ascontiguousarray(e.reshape(8, -1, 16).transpose(0, 2, 1)).reshape(128, -1).astype(np.int32)
def gcols(t, e):
    v = np.concatenate([t.reshape(8, 16, -1, 4), np.zeros((8, 16, 1, 4), BF)], axis=2)
    return np.ascontiguousarray(np.stack([v[g][:, e[g]] for g in range(8)])).reshape(128, -1)
def tile(rs):
    return np.stack(rs, axis=2).reshape(128, -1).astype(BF)
def cut(t, i, w=512):
    return t[:, w * i:w * i + w]
def pick(q, e):
    c = np.concatenate([q[0].reshape(128, -1, 4), np.zeros((128, 1, 4), np.uint8)], axis=1); s = np.concatenate([q[1], np.ones((16, 1), np.uint8)], axis=1)
    return (np.ascontiguousarray(c[:, e].reshape(128, -1)), np.ascontiguousarray(s[:, e]))
def join(*qs):
    return (np.concatenate([q[0] for q in qs], axis=1), np.concatenate([q[1] for q in qs], axis=1))
def put(q, e, v):
    c, s = q[0].reshape(128, -1, 4).copy(), q[1].copy(); c[:, e] = v[0].reshape(128, -1, 4); s[:, e] = v[1]
    return (c.reshape(128, -1), s)
def pk(c, s):
    return (np.ascontiguousarray(c), mx_ref.live(s))
def emit(q):
    return q[0], q[1]
def packed(v, rng):
    q = [mx_ref.quantize(np.ascontiguousarray(v[r])) for r in range(N)]
    return np.stack([a for a, b in q]), np.stack([mx_ref.plane(b, rng) for a, b in q])
def values_of_codes():
    e, c = np.zeros((128, 128, 4), np.float32), np.zeros((128, 2, 4), np.uint8)
    e[np.arange(128), np.arange(128), 0] = 1
    c[:127, :, 0] = np.arange(256).reshape(2, 128).T[:127]
    return mx_ref.matmul(mx_ref.quantize(e.reshape(128, 512).astype(BF)), (c.reshape(128, 8), np.full((16, 2), 127, np.uint8))).T.reshape(-1).astype(np.float64)
CODE_VALUE, SCALE_VALUE = values_of_codes(), 2.0 ** (np.arange(256) - 127.0)
def decode(q):
    return (CODE_VALUE[q[0]].reshape(16, 8, -1, 4) * SCALE_VALUE[q[1]][:, None, :, None] + 0.0).reshape(128, -1).astype(np.float32)
def f(rng, *shape):
    return mx_ref.flush((rng.standard_normal(shape, dtype=np.float32) * np.exp2(rng.integers(-2, 3, shape[:-1] + (1,)))).astype(BF))
def wide(rng, *shape, cols=0):
    v = rng.standard_normal(shape, dtype=np.float32) * np.exp2(rng.integers(-12, 13, shape)).astype(np.float32)
    if cols: v *= np.repeat(np.exp2(rng.integers(-cols, cols + 1, shape[:-2] + (1, shape[-1] // 4))) * (rng.random(shape[:-2] + (1, shape[-1] // 4)) > 0.0625), 4, axis=-1).astype(np.float32)
    return mx_ref.flush(v.astype(BF))
T, P, H = 448, 640, 3
def trim(v):
    v = v.astype(np.float32)
    v[np.abs(v) < np.float32(2.0 ** -16)] = 0
    return v.astype(BF)
def numbers_of(rng):
    return {"x": trim(f(rng, N, 128, 4 * T)), "k": trim(f(rng, N, 128, 4 * P)), "u": np.array(f(rng, N, 128, 512)), "v": np.array(f(rng, N, 128, 512))}
def weights(rng, w):
    c, p = packed(np.stack([w] * N), rng)
    return {"wc": c, "ws": p}
def still(rng):
    w = np.zeros((128, 4, 128, 4), np.float32)
    i = np.arange(128)
    for b in range(4): w[i, b, i, b] = 32
    return weights(rng, w.reshape(128, 2048).astype(BF))
def chase(nx, e):
    return {"nx": np.ascontiguousarray(nx).astype(np.int32), "st": np.stack([gtable(e[r]) for r in range(N)])}
def setup_inputs(rng):
    return {**numbers_of(rng), **weights(rng, np.array(f(rng, 128, 2048))), **chase(rng.integers(0, P, (N, 8, 2 * P)), rng.integers(0, P, (N, 8, T)))}
def setup_inputs_ties(rng):
    d = numbers_of(rng)
    x, k, u = d["x"].reshape(N, 128, T, 4), d["k"].reshape(N, 128, P, 4), d["u"].reshape(N, 128, 128, 4)
    k[:, :, ::2] = 0
    c = np.stack([rng.permutation(T) % 4 for r in range(N)])
    e = rng.integers(0, P, (N, 8, T))
    e = np.where(c[:, None, :] == 1, e // 2 * 2, e)
    for r in range(N):
        for g in rng.permutation(8)[:2]: u[r, :, 16 * g] = 0
        o = gcols(k[r].reshape(128, 4 * P), e[r]).reshape(128, T, 4)
        o = (np.float32(0.0) - o.astype(np.float32)).astype(BF)
        x[r][:, c[r] == 1] = 0
        x[r][:, c[r] == 2] = o[:, c[r] == 2]
    a = rng.integers(0, P, (N, 8, P))
    a = np.where(np.arange(P) % 2 == 0, a // 2 * 2, a)
    b = (a + 2 * rng.integers(1, P // 2, (N, 8, P))) % P
    return {"x": x.reshape(N, 128, 4 * T), "k": k.reshape(N, 128, 4 * P), "u": u.reshape(N, 128, 512), "v": d["v"], **weights(rng, np.array(f(rng, 128, 2048))), **chase(np.stack([a, b], axis=3).reshape(N, 8, 2 * P), e)}
def setup_inputs_sizes(rng):
    def columns(c):
        tiny = c % 2 == 0
        s = np.where(tiny, 2.0 ** -29, 2.0 ** 30) * np.where(c >= 2, -1.0, 1.0)
        a = 0.55 + 0.4 * rng.random((N, 128, c.shape[1], 4))
        a[:, ::16, :, 0] = np.where(tiny[:, None, :], 0.5625, a[:, ::16, :, 0])
        a[:, 8::16, :, 0] = np.where(tiny[:, None, :], 0.625, a[:, 8::16, :, 0])
        return (a * s[:, None, :, None]).astype(np.float32).astype(BF).reshape(N, 128, 4 * c.shape[1])
    d = numbers_of(rng)
    c = np.stack([rng.permutation(T) % 4 for r in range(N)])
    i = np.arange(P) % 4
    u = d["u"].reshape(N, 128, 128, 4)
    u[:, :, ::16] = 0
    for r in range(N):
        o = rng.permutation(8)
        for g in range(8):
            s = 1.0 if o[g] % 2 == 0 else -1.0
            if o[g] < 4:
                u[r, 16 * g, 16 * g, 0] = s * 1.125 * 2.0 ** -30
                u[r, 16 * g + 8, 16 * g, 0] = -s * 2.0 ** -30
            else: u[r, :, 16 * g] = (s * 2.0 ** 30 * (0.55 + 0.4 * rng.random((128, 4)))).astype(np.float32).astype(BF)
    a = 4 * rng.integers(0, P // 4, (N, 8, P)) + i
    b = (a + 4 * rng.integers(1, P // 4, (N, 8, P))) % P
    e = 4 * rng.integers(0, P // 4, (N, 8, T)) + c[:, None, :]
    return {"x": columns(c), "k": columns(np.stack([i] * N)), "u": u.reshape(N, 128, 512), "v": d["v"], **still(rng), **chase(np.stack([a, b], axis=3).reshape(N, 8, 2 * P), e)}
def setup_inputs_crowd(rng):
    d = setup_inputs(rng)
    o = rng.permutation(8)
    h = rng.permutation(N)
    full = h < N // 2
    nx, e = np.zeros((N, 8, P, 2), int), np.zeros((N, 8, T), int)
    for r in range(N):
        for g in range(8):
            nx[r, g] = rng.permutation(P)[:, None] if o[g] < 4 else rng.integers(0, 2, (P, 2)) * (P - 1)
            e[r, g] = rng.permutation(P)[:T] if full[r] else h[r] % 2 * (P - 1)
    return {**d, **chase(nx.reshape(N, 8, 2 * P), e)}
def setup_inputs_spread(rng):
    d = setup_inputs(rng)
    d["x"] = trim(wide(rng, N, 128, 4 * T, cols=6))
    d["k"] = trim(wide(rng, N, 128, 4 * P, cols=6))
    return d
def check_inputs(d):
    b = []
    for n in ("x", "k", "u", "v"):
        a = np.abs(d[n].astype(np.float32))
        if not (np.isfinite(a).all() and ((a == 0) | (a >= 2.0 ** -30) & (a <= 2.0 ** 30)).all()): b.append("a value of " + n)
    for n in ("nx", "st"):
        if ((d[n] < 0) | (d[n] >= P)).any(): b.append("an entry of " + n)
    if (d["wc"] != d["wc"][:1]).any(): b.append("wc differs between ranks")
    s = [mx_ref.live(p) for p in d["ws"]]
    if any((p != s[0]).any() for p in s): b.append("ws differs between ranks")
    return b
def reference(x, k, u, v, wc, ws, nx, st):
    w = pk(wc[0], ws[0])
    lay = [pick(w, np.arange(128 * b, 128 * b + 128)) for b in range(4)]
    qu = [mx_ref.quantize(u[r]) for r in range(N)]
    nodes = decode(join(*[mx_ref.quantize(k[r]) for r in range(N)])).astype(BF)
    now = [mx_ref.quantize(x[r]) for r in range(N)]
    p = [gentries(st[r]) for r in range(N)]
    for t in range(H):
        was = decode(join(*now))
        for r in range(N):
            m = (r + t) % N
            n = gcols(cut(nodes, m, 4 * P), p[r]).astype(np.float32)
            q = mx_ref.quantize(np.ascontiguousarray(((cut(was, r, 4 * T) + n) * np.float32(0.5)).astype(BF)))
            c = mx_ref.matmul(qu[m], q)[::16]
            p[r] = np.take_along_axis(nx[m], 2 * p[r] + (c > 0), axis=1)
            now[r] = mx_ref.quantize(tile([mx_ref.matmul(lay[b], q) * np.float32(0.03125) for b in range(4)]))
    y, pl = np.zeros((N, 128, T), np.float32), np.zeros((N, 8, T), np.float32)
    oc, osc = np.zeros((N, 128, 4 * T), np.uint8), np.zeros((N, 16, T), np.uint8)
    for r in range(N):
        y[r] = mx_ref.matmul(mx_ref.quantize(v[r]), now[r])
        pl[r] = p[r]
        oc[r], osc[r] = emit(now[r])
    return {"y": y, "pl": pl, "oc": oc, "osc": osc}

@@ -1,0 +1,413 @@
+from concourse.bass import DstId, RemoteDMATransfer
+from concourse.mybir import dt, AluOpType, ActivationFunctionType
+
+NT, NP, NH = 448, 640, 3
+SIZES = [160, 128, 160]
+HALF = 320
+CUT = 448
+TW = NP + 128
+TINY = 2.0 ** -120
+X4, U8 = "float8_e4m3fn_x4", "uint8"
+ORDER = {
+    "P": "b2_0_0:6 b3_0_0:7 b0_0_0:2 b1_0_0:0 b2_0_1:3 b0_0_1:1 b1_0_1:4 sc0_0:2 l0_0_0:6 l2_0_0:5 l1_0_0:0 b3_0_1:7 b0_0_2:4 l3_0_0:2 b1_0_2:6 b2_0_2:3 b3_0_2:4 l0_0_1:5 sc0_1:7 l2_0_1:2 l3_0_1:4 l1_0_1:3 sc0_2:1 l1_0_2:2 l0_0_2:6 l3_0_2:0 b1_1_0:5 b2_1_0:3 b0_1_0:0 b3_1_0:1 l2_0_2:5 b1_1_1:7 b3_1_1:1 sc1_0:0 l3_1_0:5 b2_1_1:4 b0_1_1:6 l0_1_0:2 l2_1_0:7 l1_1_0:3 b0_1_2:1 b3_1_2:0 b1_1_2:7 b2_1_2:1 sc1_1:6 l2_1_1:4 l1_1_1:0 l0_1_1:3 l3_1_1:5 b3_2_0:2 sc1_2:1 l2_1_2:4 l3_1_2:5 b1_2_0:7 b0_2_0:6 l0_1_2:0 b2_2_0:3 l1_1_2:2 b3_2_1:4 b1_2_1:1 b2_2_1:2 sc2_0:0 l3_2_0:4 l2_2_0:7 l1_2_0:6 b0_2_1:5 l0_2_0:1 b3_2_2:3 b2_2_2:7 b0_2_2:6 b1_2_2:2 sc2_1:4 l1_2_1:6 l3_2_1:0 l2_2_1:5 l0_2_1:3 sc2_2:4 l1_2_2:0 l2_2_2:1 l3_2_2:3 y0:7 l0_2_2:5 y1:4 y2:5",
+    "V": "mz0 mz1 df do de e0 e3 f2 zi f0 nx0 nx1 s3 f3 s1 e2 s2 s0 sn ul e1 qa f1 mi qb g2_1 g2_0 qs0_0 qn0 rt qu g1_1 qs0_1 qn1 cv3_0_0 uc cv1_0_0 cl qv0_0 g1_2 qs0_2 qn2 cv2_0_1 mg0_0 cv3_0_1 t20_0 t10_0 qv0_1 mx0_0 cv1_0_2 qs1_0 cp0_0 cr0_0_1 qv0_2 pc1_0 mg0_1 cr1_0_1 t20_1 t10_1 mg0_2 mx0_1 t10_2 cp0_1 qs1_1 t20_2 pc1_1 mx0_2 cv3_1_0 cp0_2 qv1_0 qs1_2 pc1_2 cr3_1_0 mg1_0 cv2_1_1 t21_0 t11_0 qv1_1 mx1_0 qv cp1_0 qs2_0 pc2_0 cv2_1_2 cr1_1_1 qv1_2 mg1_1 t21_1 t11_1 mx1_1 qs2_1 cp1_1 mg1_2 pc2_1 t21_2 t11_2 cv2_2_0 mx1_2 qv2_0 cp1_2 cv3_2_1 pc2_2 qs2_2 cr2_2_0 cv0_2_1 cr1_2_0 cv2_2_1 mg2_0 qv2_1 t12_0 qs3_0 cv1_2_2 qv2_2 cr3_2_1 cr2_2_1 mg2_1 mg2_2 t12_1 t12_2 qs3_1 fm1 fm0 ft qs3_2 cy2",
+    "S": "wi0 wi1 wi2 g1_0 g3_0 g0_0 g3_1 g0_2 g0_1 cv2_0_0 us cv0_0_0 bi g3_2 g2_2 cv1_0_1 sg0_0 cr0_0_0 cr1_0_0 cv0_0_1 cv0_0_2 cr2_0_0 cr3_0_0 cv2_0_2 cv3_0_2 sg0_1 cr2_0_1 pz1_0 sg0_2 cr3_0_2 cr0_0_2 cr3_0_1 cv1_1_0 cv2_1_0 pz1_1 cv0_1_0 cr2_0_2 cr1_0_2 pz1_2 cv1_1_1 sg1_0 cv3_1_1 cv0_1_1 cr2_1_0 cr0_1_0 cr1_1_0 cv0_1_2 cv3_1_2 pz2_0 cv1_1_2 sg1_1 cr2_1_1 cr3_1_1 cr0_1_1 sg1_2 cv3_2_0 cr2_1_2 pz2_1 cv1_2_0 cv0_2_0 cr1_1_2 cr0_1_2 cr3_1_2 cv1_2_1 pz2_2 sg2_0 cr3_2_0 cv3_2_2 cr0_2_0 cv0_2_2 cv2_2_2 sg2_1 cr1_2_1 cr0_2_1 sg2_2 cr1_2_2 cr2_2_2 cr3_2_2 cr0_2_2 cy0 cy1",
+}
+STORES = ["oc0 oc1 pl0 pl1 pl2 pl3 oc2 os0 y2", "y0 y1 os1 os2 os3"]
+
+SCRATCH = {
+    "ps": ("psum", [128, 4096], "float32"),
+    "kt": ("sbuf", [128, 4 * NP], "bfloat16"), "xt": ("sbuf", [128, 4 * NT], "bfloat16"), "nt": ("sbuf", [128, 4 * NT], "bfloat16"),
+    "ut": ("sbuf", [128, 512], "bfloat16"), "vtile": ("sbuf", [128, 512], "bfloat16"),
+    "quc": ("sbuf", [128, 128], X4), "qus": ("sbuf", [128, 128], U8),
+    "qvc": ("sbuf", [128, 128], X4), "qvs": ("sbuf", [128, 128], U8),
+    "wqc": ("sbuf", [128, 512], X4), "wqs": ("sbuf", [128, 512], U8),
+    "zt": ("sbuf", [128, 1544], "bfloat16"), "ia": ("sbuf", [128, 128], "float32"), "ib": ("sbuf", [128, 128], "float32"),
+    "ec": ("sbuf", [128, 1536], X4), "es": ("sbuf", [128, 1536], U8),
+    "uli": ("sbuf", [128, 8], "int32"), "ul": ("sbuf", [128, 8], "uint16"),
+    "rr": ("sbuf", [128, 192], "float32"), "rt": ("sbuf", [128, 192], "float32"),
+    "cl": ("sbuf", [128, 8], "uint16"), "bias": ("sbuf", [128, 1], "float32"),
+    "stw": ("sbuf", [128, 28], "int32"), "lst0": ("sbuf", [128, 140], "uint16"),
+    "lst1": ("sbuf", [128, 144], "uint16"), "lst2": ("sbuf", [128, 144], "uint16"),
+    "nxl": ("sbuf", [128, 80], "int32"), "nxa0": ("sbuf", [128, 80], "float32"),
+    "nxa1": ("sbuf", [128, 80], "float32"), "nxa2": ("sbuf", [128, 80], "float32"),
+    "mm": ("sbuf", [128, 512], "float16"), "tt": ("sbuf", [128, 992], "float16"), "tl": ("sbuf", [128, NT], "float16"),
+    "zc": ("sbuf", [128, 192], "float32"), "zf": ("sbuf", [128, 32], "float32"), "zo": ("sbuf", [128, 32], "float32"),
+    "ysb": ("sbuf", [128, NT], "float32"),
+    "hc": ("sbuf", [128, HALF], X4), "hs": ("sbuf", [128, HALF], U8),
+    "sc3": ("sbuf", [128, NT], X4), "ss3": ("sbuf", [128, NT], U8),
+}
+for _t in range(NH):
+    SCRATCH["tc%d" % _t] = ("sbuf", [128, TW], X4)
+    SCRATCH["ts%d" % _t] = ("sbuf", [128, TW], U8)
+    SCRATCH["win%d" % _t] = ("sbuf", [128, NP], "float32")
+    SCRATCH["pc%d" % _t] = ("sbuf", [128, 2 * NT], X4)
+    SCRATCH["pz%d" % _t] = ("sbuf", [128, 2 * NT], U8)
+    SCRATCH["sc%d" % _t] = ("sbuf", [128, NT], X4)
+    SCRATCH["ss%d" % _t] = ("sbuf", [128, NT], U8)
+    SCRATCH["vc%d" % _t] = ("sbuf", [128, NT], X4)
+    SCRATCH["vs%d" % _t] = ("sbuf", [128, NT], U8)
+    SCRATCH["bt%d" % _t] = ("sbuf", [128, 4 * NT], "bfloat16")
+    SCRATCH["lt%d" % _t] = ("sbuf", [128, 4 * NT], "bfloat16")
+    SCRATCH["sg%d" % _t] = ("sbuf", [128, NT], "bfloat16")
+
+SEMAPHORES = ["P", "V", "S", "G", "ka", "kb", "x0", "x1", "x2", "lu", "lw", "lv", "lst", "lnx", "w0", "w1", "w2",
+              "k1", "u1", "k2", "n1", "n2", "hcod", "hsca", "sent", "out"]
+
+
+def chunks():
+    return [(sum(SIZES[:c]), n) for c, n in enumerate(SIZES)]
+
+
+def list_pieces():
+    pieces, col = [], {}
+    blk = 0
+    for n in sorted(set(SIZES), reverse=True):
+        nq, nb = n // 16, n // 32
+        k = (3 * nq + 15) // 16
+        col[n] = (blk, k)
+        j = 0
+        while j < 16 * k:
+            l = min(j // nq, 2)
+            if j % 16 == 0 and nq == 8:
+                pieces.append((blk + j // 16, 0, 16, 0, (0, 0) if l == 0 else (0, 1), nb, 1 if l == 0 else 0))
+                j += 16
+                continue
+            end = min(16 * (j // 16 + 1), (l + 1) * nq if l < 2 else 16 * k)
+            pieces.append((blk + j // 16, j % 16, end - j, j - l * nq, ((0, 0), (1, 1), (0, 1))[l], nb, None))
+            j = end
+        blk += k
+    return pieces, col, blk
+
+
+def make_ops(cnt):
+    ops, CH = [], chunks()
+    A, F = AluOpType, ActivationFunctionType
+    pieces, col, nblk = list_pieces()
+    ng = 4 + 2 * len(pieces)
+
+    def add(name, eng, cost, deps, fn, ext=(), bank=None, src=None):
+        ops.append({"name": name, "eng": eng, "cost": cost, "deps": list(deps), "fn": fn, "ext": list(ext), "bank": bank, "src": src})
+
+    def move(e, on, out, in_, f=None):
+        if on == "V":
+            return e.tensor_copy(out, in_) if f is None else e.tensor_scalar(out, in_, f, None, A.mult)
+        return e.activation(out, in_, F.Copy) if f is None else e.activation(out, in_, F.Copy, scale=f)
+
+    add("mz0", "V", ("h", 516), [], lambda e, T, k, on: e.memset(T.zt[:, 0:516], 0.0))
+    add("mz1", "V", ("h", 1028), [], lambda e, T, k, on: e.memset(T.zt[:, 516:1544], 0.0))
+    add("df", "V", ("c", 128), ["mz0"], lambda e, T, k, on: e.tensor_scalar(T.zt[:, 3:515:4], T.ib[:], 0.0, None, A.is_equal), [("G", 1)])
+    add("de", "V", ("c", 128), ["mz1"], lambda e, T, k, on: e.tensor_scalar(T.zt[:, 519:1031:4], T.ia[:], 0.0, None, A.is_equal), [("G", 2)])
+    add("do", "V", ("c", 128), ["mz1"], lambda e, T, k, on: e.tensor_scalar(T.zt[:, 1031:1543:4], T.ia[:], 1000.0, None, A.is_equal), [("G", 2)])
+    for b in range(4):
+        add("e%d" % b, "V", ("q", 128), ["df"], lambda e, T, k, on, b=b: e.quantize_mx(T.ec[:, 128 * b:128 * b + 128], T.es[:, 128 * b:128 * b + 128], T.zt[:, 3 - b:515 - b]))
+        add("f%d" % b, "V", ("q", 256), ["de", "do"], lambda e, T, k, on, b=b:
+            e.quantize_mx(T.ec[:, 512 + 256 * b:768 + 256 * b], T.es[:, 512 + 256 * b:768 + 256 * b], T.zt[:, 519 - b:1543 - b]))
+    for t in range(NH):
+        add("wi%d" % t, "S", ("c", NP), ["de", "do"], lambda e, T, k, on, t=t: e.activation(T["win%d" % t][:], T.zt[:, 516:516 + NP], F.Copy))
+    add("mi", "V", ("h", 512), ["df"], lambda e, T, k, on: e.tensor_copy(T.mm[:], T.zt[:, 0:512]))
+    add("zi", "V", ("c", 4), [], lambda e, T, k, on: e.memset(T.zf[:, 28:32], 0.0))
+    for b in range(2):
+        add("nx%d" % b, "V", ("c", 40), [], lambda e, T, k, on, b=b: e.tensor_copy(T.nxa0[:, 40 * b:40 * b + 40], T.nxl[:, b:80:2]), [("lnx", 16)])
+    for b in range(4):
+        add("s%d" % b, "V", ("c", 28), [], lambda e, T, k, on, b=b: e.tensor_scalar(T.lst0[:, 28 * b:28 * b + 28], T.stw[:], 4.0, float(b), A.mult, A.add), [("lst", 16)])
+    add("sn", "V", ("c", 28), [], lambda e, T, k, on: e.tensor_copy(T.lst0[:, 112:140], T.stw[:]), [("lst", 16)])
+    add("qa", "V", ("q", HALF), [], lambda e, T, k, on: e.quantize_mx(T.tc0[:, 0:HALF], T.ts0[:, 0:HALF], T.kt[:, 0:4 * HALF]), [("ka", 16)])
+    add("qb", "V", ("q", NP - HALF), [], lambda e, T, k, on: e.quantize_mx(T.tc0[:, HALF:NP], T.ts0[:, HALF:NP], T.kt[:, 4 * HALF:4 * NP]), [("kb", 16)])
+    add("qu", "V", ("q", 128), [], lambda e, T, k, on: e.quantize_mx(T.quc[:], T.qus[:], T.ut[:]), [("lu", 16)])
+    add("qv", "V", ("q", 128), [], lambda e, T, k, on: e.quantize_mx(T.qvc[:], T.qvs[:], T.vtile[:]), [("lv", 16)])
+    add("ul", "V", ("c", 8), [], lambda e, T, k, on: e.tensor_copy(T.ul[:], T.uli[:]), [("G", 3)])
+    add("uc", "V", ("g", 128), ["qu", "ul"], lambda e, T, k, on: e.tensor_copy(T.tc0[:, NP:TW].bitcast(dt.uint32), T.quc[:].bitcast(dt.uint32).indirect(T.ul[:, 0:8])))
+    add("us", "F", ("g", 128), ["qu", "ul"], lambda e, T, k, on: move(e, on, T.ts0[:, NP:TW], T.qus[:].indirect(T.ul[:, 0:8])))
+    w = 32 * nblk
+    add("rt", "V", ("c", w + 32), [], lambda e, T, k, on: e.transpose(T.rt[:, 0:w + 32], T.rr[:, 0:w + 32]), [("G", ng)])
+    add("cl", "V", ("c", 4), ["rt"], lambda e, T, k, on: e.tensor_scalar(T.cl[:, 0:nblk], T.rt[:, 0:w:32], float(max(SIZES) // 8 + 1), None, A.min))
+    add("bi", "S", ("c", 1), ["rt"], lambda e, T, k, on: e.activation(T.bias[:], T.rt[:, w:w + 1], F.Copy, scale=-TINY))
+    for c, (o, n) in enumerate(CH):
+        add("qs0_%d" % c, "V", ("q", n), [], lambda e, T, k, on, o=o, n=n: e.quantize_mx(T.sc0[:, o:o + n], T.ss0[:, o:o + n], T.xt[:, 4 * o:4 * (o + n)]), [("x%d" % c, 16)])
+
+    for t in range(NH):
+        tab = {0: [], 1: [("k1", cnt["k1"])], 2: [("k2", cnt["k2"])]}[t]
+        utab = {0: [], 1: [("u1", cnt["u1"])], 2: tab}[t]
+        for c, (o, n) in enumerate(CH):
+            s, nq, q0, nb = "%d_%d" % (t, c), n // 16, o // 16, n // 32
+            tc, ts, pc, pz, ls = "tc%d" % t, "ts%d" % t, "pc%d" % t, "pz%d" % t, "lst%d" % t
+            if t == 0:
+                for b in range(4):
+                    add("g%d_%d" % (b, c), "F", ("g", n), ["s%d" % b], lambda e, T, k, on, b=b, o=o, n=n, q0=q0, nq=nq:
+                        move(e, on, T.nt[:, 4 * o + b:4 * (o + n):4], T.kt[:].indirect(T.lst0[:, 28 * b + q0:28 * b + q0 + nq])), [("ka", 16), ("kb", 16)])
+                add("qn%d" % c, "V", ("q", n), ["g%d_%d" % (b, c) for b in range(4)], lambda e, T, k, on, o=o, n=n:
+                    e.quantize_mx(T.pc0[:, o:o + n], T.pz0[:, o:o + n], T.nt[:, 4 * o:4 * (o + n)]))
+                pn, ndep, nat = ["qn%d" % c], ["sn"], 112 + q0
+            else:
+                ndep, nat, l = ["cp%d_%d" % (t - 1, c)], 48 * c + 2 * nq, 48 * c
+                add("pc" + s, "V", ("g", 2 * n), ndep, lambda e, T, k, on, o=o, n=n, l=l, tc=tc, pc=pc, ls=ls:
+                    e.tensor_copy(T[pc][:, 2 * o:2 * (o + n)].bitcast(dt.uint32), T[tc][:, 0:NP].bitcast(dt.uint32).indirect(T[ls][:, l:l + n // 8])), tab)
+                add("pz" + s, "F", ("g", 2 * n), ndep, lambda e, T, k, on, o=o, n=n, l=l, ts=ts, pz=pz, ls=ls:
+                    move(e, on, T[pz][:, 2 * o:2 * (o + n)], T[ts][:, 0:NP].indirect(T[ls][:, l:l + n // 8])), tab)
+                pn = ["pc" + s, "pz" + s]
+            for b in range(4):
+                def blend(e, T, k, on, b=b, t=t, o=o, n=n, pc=pc, pz=pz):
+                    out = T.ps[:, 512 * k:512 * k + n]
+                    eb = 128 * b
+                    e.matmul_mx(out, T.ec[:, eb:eb + 128], T.es[:, eb:eb + 128], T["sc%d" % t][:, o:o + n], T["ss%d" % t][:, o:o + n], True, False)
+                    if t == 0:
+                        return e.matmul_mx(out, T.ec[:, eb:eb + 128], T.es[:, eb:eb + 128], T.pc0[:, o:o + n], T.pz0[:, o:o + n], False, True)
+                    eb = 512 + 256 * b
+                    e.matmul_mx(out, T.ec[:, eb:eb + 128], T.es[:, eb:eb + 128], T[pc][:, 2 * o:2 * o + n], T[pz][:, 2 * o:2 * o + n], False, False)
+                    return e.matmul_mx(out, T.ec[:, eb + 128:eb + 256], T.es[:, eb + 128:eb + 256], T[pc][:, 2 * o + n:2 * o + 2 * n], T[pz][:, 2 * o + n:2 * o + 2 * n], False, True)
+                add("b%d_%s" % (b, s), "P", ("p3" if t else "p2", n), pn + ["qs" + s, "e%d" % b] + (["f%d" % b] if t else []), blend, bank=True)
+                add("cv%d_%s" % (b, s), "F", ("c", n), ["b%d_%s" % (b, s)], lambda e, T, k, on, b=b, t=t, o=o, n=n:
+                    move(e, on, T["bt%d" % t][:, 4 * o + b:4 * (o + n):4], T.ps[:, 512 * k:512 * k + n], 0.5), src="b%d_%s" % (b, s))
+            add("qv" + s, "V", ("q", n), ["cv%d_%s" % (b, s) for b in range(4)], lambda e, T, k, on, t=t, o=o, n=n:
+                e.quantize_mx(T["vc%d" % t][:, o:o + n], T["vs%d" % t][:, o:o + n], T["bt%d" % t][:, 4 * o:4 * (o + n)]))
+            add("sc" + s, "P", ("p1", n), ["qv" + s] + (["uc", "us"] if t == 0 else []), lambda e, T, k, on, t=t, o=o, n=n, tc=tc, ts=ts:
+                e.matmul_mx(T.ps[:, 512 * k:512 * k + n], T[tc][:, NP:TW], T[ts][:, NP:TW], T["vc%d" % t][:, o:o + n], T["vs%d" % t][:, o:o + n], True, True), utab, bank=True)
+            for b in range(4):
+                add("l%d_%s" % (b, s), "P", ("p1", n), ["qv" + s], lambda e, T, k, on, b=b, t=t, o=o, n=n:
+                    e.matmul_mx(T.ps[:, 512 * k:512 * k + n], T.wqc[:, 128 * b:128 * b + 128], T.wqs[:, 128 * b:128 * b + 128], T["vc%d" % t][:, o:o + n], T["vs%d" % t][:, o:o + n], True, True),
+                    [("lw", 32)], bank=True)
+                add("cr%d_%s" % (b, s), "F", ("c", n), ["l%d_%s" % (b, s)], lambda e, T, k, on, b=b, t=t, o=o, n=n:
+                    move(e, on, T["lt%d" % t][:, 4 * o + b:4 * (o + n):4], T.ps[:, 512 * k:512 * k + n], 0.03125), src="l%d_%s" % (b, s))
+            add("qs%d_%d" % (t + 1, c), "V", ("q", n), ["cr%d_%s" % (b, s) for b in range(4)], lambda e, T, k, on, t=t, o=o, n=n:
+                e.quantize_mx(T["sc%d" % (t + 1)][:, o:o + n], T["ss%d" % (t + 1)][:, o:o + n], T["lt%d" % t][:, 4 * o:4 * (o + n)]))
+            add("sg" + s, "S", ("c", n), ["sc" + s, "bi"], lambda e, T, k, on, t=t, o=o, n=n:
+                e.activation(T["sg%d" % t][:, o:o + n], T.ps[:, 512 * k:512 * k + n], F.Sign, bias=T.bias[:, 0:1], scale=T.rt[:, w:w + 1]), src="sc" + s)
+            m = o + 16 * (c + 1)
+            add("mg" + s, "V", ("g", n), ["sg" + s, "mi"] + ndep, lambda e, T, k, on, t=t, o=o, n=n, m=m, ls=ls, nat=nat, nq=nq:
+                e.tensor_tensor(T.mm[:, m:m + n], T["win%d" % t][:].indirect(T[ls][:, nat:nat + nq]), T["sg%d" % t][:, o:o + n], A.mult), [("w%d" % t, 32)])
+            if t < NH - 1:
+                z, to = 96 * t + 32 * c, 2 * o + 32 * c
+                lc, lk = col[n]
+                add("t1" + s, "V", ("h", n), ["mg" + s], lambda e, T, k, on, n=n, m=m, to=to: e.transpose(T.tt[:, to:to + n], T.mm[:, m:m + n]))
+                add("t2" + s, "V", ("h", n + 32), ["mg" + s], lambda e, T, k, on, n=n, m=m, to=to: e.transpose(T.tt[:, to + n:to + 2 * n + 32], T.mm[:, m - 16:m + n + 16]))
+                add("mx" + s, "V", ("c", 8 * nb + 4), ["t1" + s, "t2" + s], lambda e, T, k, on, n=n, to=to, z=z, nb=nb:
+                    e.tensor_tensor(T.zc[:, z:z + 4 * nb + 2], T.tt[:, to:to + 2 * n + 32:16], T.tt[:, to + 1:to + 2 * n + 32:16], A.max))
+                add("cp" + s, "V", ("g", 16 * lk), ["mx" + s, "cl"], lambda e, T, k, on, t=t, c=c, z=z, nb=nb, lc=lc, lk=lk:
+                    e.tensor_copy(T["lst%d" % (t + 1)][:, 48 * c:48 * c + 16 * lk], T.zc[:, z:z + 4 * nb + 2].indirect(T.cl[:, lc:lc + lk])))
+            else:
+                add("t1" + s, "V", ("h", n), ["mg" + s], lambda e, T, k, on, o=o, n=n, m=m: e.transpose(T.tl[:, o:o + n], T.mm[:, m:m + n]))
+                add("y%d" % c, "P", ("p1", n), ["qs3_%d" % c, "qv"], lambda e, T, k, on, o=o, n=n:
+                    e.matmul_mx(T.ps[:, 512 * k:512 * k + n], T.qvc[:], T.qvs[:], T.sc3[:, o:o + n], T.ss3[:, o:o + n], True, True), bank=True)
+                add("cy%d" % c, "F", ("c", n), ["y%d" % c], lambda e, T, k, on, o=o, n=n: move(e, on, T.ysb[:, o:o + n], T.ps[:, 512 * k:512 * k + n]), src="y%d" % c)
+    tl = ["t1%d_%d" % (NH - 1, c) for c in range(len(CH))]
+    for h in range(2):
+        add("fm%d" % h, "V", ("c", 28), tl, lambda e, T, k, on, h=h: e.tensor_tensor(T.zf[:, 14 * h:14 * h + 14], T.tl[:, 16 * h:NT:32], T.tl[:, 16 * h + 1:NT:32], A.max))
+    add("ft", "V", ("c", 32), ["fm0", "fm1", "zi"], lambda e, T, k, on: e.transpose(T.zo[:], T.zf[:]))
+    return ops
+
+
+def bits(engines):
+    return sum(1 << e for e in engines)
+
+
+def plan(T, topo):
+    cores, n = list(T.cores), len(T.cores)
+    calls, got = {}, {}
+
+    def put(src, item):
+        calls.setdefault(src, []).append(item)
+
+    def send(src, dst, a, b, c0, c1, sem, eng):
+        for kind in "cs":
+            s = sem if isinstance(sem, str) else sem[kind]
+            put(src, ("send", dst, kind, a, b, c0, c1, s, eng))
+            got[(dst, s)] = got.get((dst, s), 0) + len(eng)
+            got[(src, "sent")] = got.get((src, "sent"), 0) + len(eng)
+
+    for r in range(n):
+        me, d1, d2 = cores[r], cores[(r - 1) % n], cores[(r - 2) % n]
+        near = topo.chip(d1) == topo.chip(me)
+        off = topo.engines(me, d2)
+        other = [c for c in topo.cores_of(me) if c != me][0]
+        rest = [e for e in topo.engines(me, other) if e not in off]
+        e1, e2 = (rest, off) if near else (off[:len(off) // 2], off[len(off) // 2:])
+        put(me, ("nx", d1, d2, e1, e2))
+        got[(d1, "n1")], got[(d2, "n2")] = len(e1), len(e2)
+        got[(me, "sent")] = got.get((me, "sent"), 0) + len(e1) + len(e2)
+        put(me, ("wait", ["qa"]))
+        if near:
+            first = topo.engines(me, d1)
+            send(me, d1, "t0", "t1", 0, HALF, "k1", first)
+        else:
+            first = off
+            h = [c for c in topo.cores_of(me) if c not in cores and topo.die(c) != topo.die(me) and topo.may_write(c, d1)][0]
+            send(me, h, "t0", "h", 0, HALF, {"c": "hcod", "s": "hsca"}, rest)
+            send(h, d1, "h", "t1", 0, HALF, "k1", topo.engines(h, d1))
+            calls[h] = [("sem", "hcod"), calls[h][0], ("sem", "hsca"), calls[h][1]]
+        put(me, ("iota", 0))
+        put(me, ("wait", ["qb"]))
+        send(me, d1, "t0", "t1", HALF, NP, "k1", first)
+        put(me, ("iota", 1))
+        put(me, ("wait", ["uc", "us"]))
+        send(me, d1, "t0", "t1", NP, TW, "u1", first)
+        put(me, ("sem", "k1"))
+        if near:
+            send(me, d2, "t0", "t2", 0, CUT, "k2", off)
+            put(me, ("sem", "u1"))
+            send(me, d1, "t1", "t2", 0, TW, "k2", rest)
+        else:
+            put(me, ("sem", "u1"))
+            send(me, d1, "t1", "t2", CUT, TW, "k2", off)
+    return calls, got
+
+
+BUF = {"t0": ("tc0", "ts0"), "t1": ("tc1", "ts1"), "t2": ("tc2", "ts2"), "h": ("hc", "hs")}
+
+
+def list_rows(g, T, blk, j0, ln, q, hs, nb, rep):
+    for u in range(2):
+        base, step = (q + hs[u], 2 * nb + 2) if u == 0 else (2 * nb + q + hs[u], -2 * nb)
+        pat = [[2, ln // 2], [step, 2]] if rep is None else [[rep, 2], [2, ln // 4], [step, 2]]
+        a = 32 * blk + 16 * u + j0
+        g.iota(T.rr[:, a:a + ln], pat, base, 0, allow_small_or_imprecise_dtypes=True).then_inc(T.sem.G, 1)
+
+
+def waits(order, idx, by, before):
+    know, seen, out = {e: {} for e in order}, {}, {}
+    pos = {e: 0 for e in order}
+    while len(out) < len(idx):
+        for e in order:
+            while pos[e] < len(order[e]):
+                n = order[e][pos[e]]
+                ds = by[n]["deps"] + ([before[n]] if n in before else [])
+                if any(d not in out for d in ds):
+                    break
+                want = {}
+                for d in ds:
+                    want[idx[d][0]] = max(want.get(idx[d][0], 0), idx[d][1])
+                for s, v in by[n]["ext"]:
+                    want[s] = max(want.get(s, 0), v)
+                want = {s: v for s, v in want.items() if know[e].get(s, 0) < v}
+                for s in list(want):
+                    if any(o != s and o in order and seen[(o, want[o])].get(s, 0) >= want[s] for o in want):
+                        del want[s]
+                for s, v in want.items():
+                    for s2, v2 in list(seen.get((s, v), {}).items()) + [(s, v)]:
+                        know[e][s2] = max(know[e].get(s2, 0), v2)
+                out[n] = want
+                seen[idx[n]] = dict(know[e])
+                pos[e] += 1
+    return out
+
+
+def rank_program(g, core, T, topo):
+    calls, got = plan(T, topo)
+    rank = T.rank_of(core)
+    sem, CH = T.sem, chunks()
+    idx = {}
+    pieces, col, nblk = list_pieces()
+    late = pieces[4:]
+    if rank is not None:
+        ops = make_ops({s: got[(core, s)] for s in ("k1", "u1", "k2")})
+        by = {o["name"]: o for o in ops}
+        order, bank, before = {}, {}, {}
+        for e in ORDER:
+            order[e] = [x.split(":")[0] for x in ORDER[e].split()]
+            for i, n in enumerate(order[e]):
+                idx[n] = (e, i + 1)
+        reader = {o["src"]: o["name"] for o in ops if o["src"]}
+        last = {}
+        for x in ORDER["P"].split():
+            n, k = x.split(":")
+            bank[n] = bank[reader[n]] = int(k)
+            if k in last:
+                before[n] = last[k]
+            last[k] = reader[n]
+        todo = waits(order, idx, by, before)
+
+        def waiter(q):
+            seen = {}
+
+            def need(s, v):
+                if seen.get(s, 0) < v:
+                    q.wait_ge(sem[s], v)
+                    seen[s] = v
+            return need
+
+        sy, sc = g.sync, g.scalar
+        sc.dma_start(T.nxl[:], T.nx[:]).then_inc(sem.lnx, 16)
+        sy.dma_start(T.kt[:, 0:4 * HALF], T.k[:, 0:4 * HALF]).then_inc(sem.ka, 16)
+        sy.dma_start(T.kt[:, 4 * HALF:4 * NP], T.k[:, 4 * HALF:4 * NP]).then_inc(sem.kb, 16)
+        sc.dma_start(T.stw[:], T.st[:]).then_inc(sem.lst, 16)
+        xs = [(T.xt[:, 4 * o:4 * (o + n)], T.x[:, 4 * o:4 * (o + n)]) for o, n in CH]
+        sy.dma_start(*xs[0]).then_inc(sem.x0, 16)
+        sy.dma_start(T.ut[:], T.u[:]).then_inc(sem.lu, 16)
+        sy.dma_start(*xs[1]).then_inc(sem.x1, 16)
+        sy.dma_start(T.wqc[:].bitcast(dt.uint8), T.wc[:]).then_inc(sem.lw, 16)
+        sy.dma_start(T.wqs[:], T.ws[:]).then_inc(sem.lw, 16)
+        if len(CH) > 2:
+            sy.dma_start(*xs[2]).then_inc(sem.x2, 16)
+        ns = waiter(sy)
+        for t in range(NH):
+            ns(*idx["wi%d" % t])
+            if t == 0:
+                ns(*idx["nx0"])
+                ns(*idx["nx1"])
+            else:
+                ns("n%d" % t, got[(core, "n%d" % t)])
+            for b in range(2):
+                sy.dma_start(T["win%d" % t][b:128:16, :], T["nxa%d" % t][:, 40 * b:40 * b + 40]).then_inc(sem["w%d" % t], 16)
+        sy.dma_start(T.vtile[:], T.v[:]).then_inc(sem.lv, 16)
+
+        stores = {}
+        for c, (o, n) in enumerate(CH):
+            stores["oc%d" % c] = (["qs3_%d" % c], T.oc[:, 4 * o:4 * (o + n)], T.sc3[:, o:o + n].bitcast(dt.uint8))
+            stores["y%d" % c] = (["cy%d" % c], T.y[:, o:o + n], T.ysb[:, o:o + n])
+        for a in range(4):
+            stores["os%d" % a] = (["qs3_%d" % c for c in range(len(CH))], T.osc[4 * a:4 * a + 4, :], T.ss3[32 * a:32 * a + 4, :])
+            stores["pl%d" % a] = (["ft"], T.pl[2 * a:2 * a + 2, :], T.zo[32 * a:32 * a + 28, :])
+
+        def store(q, need, names):
+            for x in names.split():
+                ds, dst, src = stores[x]
+                for e in order:
+                    need(e, max([0] + [idx[d][1] for d in ds if idx[d][0] == e]))
+                q.dma_start(dst, src).then_inc(sem.out, 16)
+
+        for e, q in (("P", g.tensor), ("V", g.vector), ("S", g.scalar)):
+            for n in order[e]:
+                for s, v in todo[n].items():
+                    q.wait_ge(sem[s], v)
+                by[n]["fn"](q, T, bank.get(n), e).then_inc(sem[e], 1)
+            if e == "S":
+                store(q, waiter(q), STORES[1])
+        store(sy, ns, STORES[0])
+        for e in order:
+            ns(e, len(order[e]))
+        ns("out", 16 * len(stores))
+
+        flag = {"allow_small_or_imprecise_dtypes": True}
+        g.iota(T.ib[:], [[-1, 128]], 0, 1, **flag).then_inc(sem.G, 1)
+        g.iota(T.ia[:], [[-32, 4], [984, 2], [-1, 16]], 0, 1, **flag).then_inc(sem.G, 1)
+        g.iota(T.uli[:], [[16, 8]], 0, 0).then_inc(sem.G, 1)
+        g.iota(T.rr[:, 32 * nblk:32 * nblk + 32], [[0, 16], [2, 2]], -1, 0, **flag).then_inc(sem.G, 1)
+        for p in pieces[:4]:
+            list_rows(g, T, *p)
+
+    for it in calls.get(core, []):
+        if it[0] == "nx":
+            g.wait_ge(sem.V, max(idx["nx0"][1], idx["nx1"][1]))
+            tr = []
+            for d, eng, name in ((it[1], it[3], "1"), (it[2], it[4], "2")):
+                rid, pid, se = topo.addr(d)
+                tr.append(RemoteDMATransfer(dst_ids=[DstId(rid=rid, pnc=pid)], dma_engine_mask=bits(eng), remote_sem=sem["n" + name], src=T.nxa0[:], dst=T["nxa" + name][:]))
+            g.remote_dma_fused(tr, local_sem=sem.sent)
+        elif it[0] == "wait":
+            for d in it[1]:
+                g.wait_ge(sem[idx[d][0]], idx[d][1])
+        elif it[0] == "sem":
+            g.wait_ge(sem[it[1]], got[(core, it[1])])
+        elif it[0] == "iota":
+            for p in late[it[1]::2]:
+                list_rows(g, T, *p)
+        else:
+            x, d, kind, a, b, c0, c1, s, eng = it
+            rid, pid, se = topo.addr(d)
+            i = 0 if kind == "c" else 1
+            src, dst = T[BUF[a][i]][:, c0:c1], T[BUF[b][i]][:, c0:c1]
+            if kind == "c":
+                src, dst = src.bitcast(dt.uint8), dst.bitcast(dt.uint8)
+            g.remote_dma(dst, src, sem[s], sem.sent, pid, rid, bits(eng))
+    if (core, "sent") in got:
+        g.wait_ge(sem.sent, got[(core, "sent")])

@@ -2,37 +2,36 @@ from concourse.bass import DstId, RemoteDMATransfer
 from concourse.mybir import dt, AluOpType, ActivationFunctionType
 
 NT, NP, NH = 448, 640, 3
-SIZES = [160, 128, 160]
+SIZES = [160, 160, 128]
 HALF = 320
 CUT = 448
 TW = NP + 128
 TINY = 2.0 ** -120
 X4, U8 = "float8_e4m3fn_x4", "uint8"
-ORDER = {
-    "P": "b2_0_0:6 b3_0_0:7 b0_0_0:2 b1_0_0:0 b2_0_1:3 b0_0_1:1 b1_0_1:4 sc0_0:2 l0_0_0:6 l2_0_0:5 l1_0_0:0 b3_0_1:7 b0_0_2:4 l3_0_0:2 b1_0_2:6 b2_0_2:3 b3_0_2:4 l0_0_1:5 sc0_1:7 l2_0_1:2 l3_0_1:4 l1_0_1:3 sc0_2:1 l1_0_2:2 l0_0_2:6 l3_0_2:0 b1_1_0:5 b2_1_0:3 b0_1_0:0 b3_1_0:1 l2_0_2:5 b1_1_1:7 b3_1_1:1 sc1_0:0 l3_1_0:5 b2_1_1:4 b0_1_1:6 l0_1_0:2 l2_1_0:7 l1_1_0:3 b0_1_2:1 b3_1_2:0 b1_1_2:7 b2_1_2:1 sc1_1:6 l2_1_1:4 l1_1_1:0 l0_1_1:3 l3_1_1:5 b3_2_0:2 sc1_2:1 l2_1_2:4 l3_1_2:5 b1_2_0:7 b0_2_0:6 l0_1_2:0 b2_2_0:3 l1_1_2:2 b3_2_1:4 b1_2_1:1 b2_2_1:2 sc2_0:0 l3_2_0:4 l2_2_0:7 l1_2_0:6 b0_2_1:5 l0_2_0:1 b3_2_2:3 b2_2_2:7 b0_2_2:6 b1_2_2:2 sc2_1:4 l1_2_1:6 l3_2_1:0 l2_2_1:5 l0_2_1:3 sc2_2:4 l1_2_2:0 l2_2_2:1 l3_2_2:3 y0:7 l0_2_2:5 y1:4 y2:5",
-    "V": "mz0 mz1 df do de e0 e3 f2 zi f0 nx0 nx1 s3 f3 s1 e2 s2 s0 sn ul e1 qa f1 mi qb g2_1 g2_0 qs0_0 qn0 rt qu g1_1 qs0_1 qn1 cv3_0_0 uc cv1_0_0 cl qv0_0 g1_2 qs0_2 qn2 cv2_0_1 mg0_0 cv3_0_1 t20_0 t10_0 qv0_1 mx0_0 cv1_0_2 qs1_0 cp0_0 cr0_0_1 qv0_2 pc1_0 mg0_1 cr1_0_1 t20_1 t10_1 mg0_2 mx0_1 t10_2 cp0_1 qs1_1 t20_2 pc1_1 mx0_2 cv3_1_0 cp0_2 qv1_0 qs1_2 pc1_2 cr3_1_0 mg1_0 cv2_1_1 t21_0 t11_0 qv1_1 mx1_0 qv cp1_0 qs2_0 pc2_0 cv2_1_2 cr1_1_1 qv1_2 mg1_1 t21_1 t11_1 mx1_1 qs2_1 cp1_1 mg1_2 pc2_1 t21_2 t11_2 cv2_2_0 mx1_2 qv2_0 cp1_2 cv3_2_1 pc2_2 qs2_2 cr2_2_0 cv0_2_1 cr1_2_0 cv2_2_1 mg2_0 qv2_1 t12_0 qs3_0 cv1_2_2 qv2_2 cr3_2_1 cr2_2_1 mg2_1 mg2_2 t12_1 t12_2 qs3_1 fm1 fm0 ft qs3_2 cy2",
-    "S": "wi0 wi1 wi2 g1_0 g3_0 g0_0 g3_1 g0_2 g0_1 cv2_0_0 us cv0_0_0 bi g3_2 g2_2 cv1_0_1 sg0_0 cr0_0_0 cr1_0_0 cv0_0_1 cv0_0_2 cr2_0_0 cr3_0_0 cv2_0_2 cv3_0_2 sg0_1 cr2_0_1 pz1_0 sg0_2 cr3_0_2 cr0_0_2 cr3_0_1 cv1_1_0 cv2_1_0 pz1_1 cv0_1_0 cr2_0_2 cr1_0_2 pz1_2 cv1_1_1 sg1_0 cv3_1_1 cv0_1_1 cr2_1_0 cr0_1_0 cr1_1_0 cv0_1_2 cv3_1_2 pz2_0 cv1_1_2 sg1_1 cr2_1_1 cr3_1_1 cr0_1_1 sg1_2 cv3_2_0 cr2_1_2 pz2_1 cv1_2_0 cv0_2_0 cr1_1_2 cr0_1_2 cr3_1_2 cv1_2_1 pz2_2 sg2_0 cr3_2_0 cv3_2_2 cr0_2_0 cv0_2_2 cv2_2_2 sg2_1 cr1_2_1 cr0_2_1 sg2_2 cr1_2_2 cr2_2_2 cr3_2_2 cr0_2_2 cy0 cy1",
-}
-STORES = ["oc0 oc1 pl0 pl1 pl2 pl3 oc2 os0 y2", "y0 y1 os1 os2 os3"]
+ORDER = "mz df ra do zi e0 de* e3 f3 wi1 wi0 nh s0 s3 nx1 nx0 s2 e1 s1 e2 qa f2 f0 f1 g0_0 g1_0 g2_0 g3_0* qb qs0_0 qn0 rb g0_1* g2_1 g3_1 g1_1 a3_0_0 a2_0_0 qs0_1 n3_0_0 cv3_0_0 n2_0_0 a0_0_0 n0_0_0 n1_0_0 a1_0_0 cv2_0_0 cv0_0_0 cv1_0_0 cl160 qn1 a1_0_1 n1_0_1 a0_0_1 g2_2 g3_2 cv1_0_1 qu g0_2* mi n0_0_1 a2_0_1 n2_0_1 n3_0_1 a3_0_1 cv2_0_1 qv0_0 sc0_0 g1_2* bi sn qs0_2 qn2 cv0_0_1* sg0_0 cv3_0_1 l3_0_0 l2_0_0 cr2_0_0* l0_0_0 a0_0_2 l1_0_0 n0_0_2 a3_0_2 n1_0_2 a2_0_2 a1_0_2 cr0_0_0 cr1_0_0 cr3_0_0 n2_0_2 n3_0_2 cv0_0_2 cv1_0_2 cv2_0_2 mg0_0 qv0_1 t20_0 t10_0 qs1_0 mx0_0 cv3_0_2* cp0_0 cl128 sc0_1 l3_0_1 sg0_1 qv0_2 cr3_0_1 l1_0_1 l0_0_1 pz1_0 mg0_1 pc1_0 t10_1 t20_1 a1_1_0 l2_0_1 cr2_0_1 a3_1_0 sc0_2 sg0_2 cr0_0_1 l0_0_2 l3_0_2 n2_1_0 n3_1_0 cr1_0_1 a0_1_0 n1_1_0 n0_1_0 a2_1_0 l1_0_2 cr3_0_2* mx0_1 mg0_2 cr0_0_2 cp0_1 qs1_1 cv3_1_0 t10_2 t20_2 pc1_1 mx0_2 cv1_1_0* pz1_1 cp0_2 a3_1_1 l2_0_2 a1_1_1 a2_1_1 cv2_1_0 cv0_1_0 qv1_0 cr2_0_2 cr1_0_2 pz1_2 n3_1_1 n1_1_1 a0_1_1 sc1_0 pc1_2 cv3_1_1* qs1_2 sg1_0 l0_1_0 n0_1_1 l1_1_0 l3_1_0 cr0_1_0 l2_1_0 n2_1_1 a0_1_2 a3_1_2 cr1_1_0 cv0_1_1 cv1_1_1 mg1_0 cr2_1_0 cr3_1_0* t11_0 t21_0 cv2_1_1* mx1_0 qv1_1 cp1_0 qs2_0 a1_1_2 n3_1_2 cv3_1_2 n0_1_2 cv0_1_2 n1_1_2 a2_1_2 n2_1_2 pc2_0 cv1_1_2 pz2_0 cv2_1_2* qv qv1_2 sc1_1 l3_1_1 l2_1_1 l1_1_1 a1_2_0 l0_1_1 n3_2_0 a3_2_0 sg1_1 cr2_1_1 cr1_1_1 cr0_1_1 n1_2_0 cv3_2_0 sc1_2 l2_1_2 l0_1_2 a2_2_0 n2_2_0 l3_1_2 cr2_1_2 sg1_2 cv1_2_0 mg1_1 cr3_1_1* t11_1 t21_1 qs2_1 mx1_1 cp1_1 mg1_2 cv2_2_0 pz2_1 a1_2_1 a0_2_0 a3_2_1 n0_2_0 l1_1_2 a2_2_1 a0_2_1 pc2_1 t21_2 t11_2 cr0_1_2* mx1_2 cv0_2_0 qv2_0 cp1_2 n1_2_1 n3_2_1 n2_2_1 cr3_1_2 cr1_1_2 qs2_2 cv1_2_1* pc2_2 cv3_2_1 pz2_2 l3_2_0 l0_2_0 n0_2_1 l2_2_0 a3_2_2 sc2_0 cr3_2_0* cv2_2_1 cv0_2_1 cr2_2_0* cr0_2_0* sg2_0 a2_2_2 n2_2_2 l1_2_0 a0_2_2 qv2_1 cv2_2_2 mg2_0 cr1_2_0 n1_2_2 n3_2_2 a1_2_2 n0_2_2 cv1_2_2 qs3_0 cv3_2_2* t12_0 cv0_2_2 l0_2_1 cr0_2_1* qv2_2 sc2_1 sg2_1 l1_2_1 l3_2_1 cr3_2_1* mg2_1 l2_2_1 cr1_2_1 cr2_2_1 sc2_2 l3_2_2 sg2_2 l0_2_2 l1_2_2 l2_2_2 y0 qs3_1 cr0_2_2* mg2_2 t12_1 cr3_2_2 cr1_2_2 cr2_2_2 qs3_2 y1 t12_2 fm1 fm0 y2 cy2* cy1 ft cy0"
+LOADS = "ka kb x0 u x1 W x2 w0 w1 v w2"
+STORES = ["oc0 oc1 y1 oc2 os1 os3 y2 pl1 pl3", "y0 os0 os2 pl0 pl2"]
+EARLY = 12
+KINDS = sorted(set(SIZES), reverse=True)
+NC = len(SIZES)
 
 SCRATCH = {
     "ps": ("psum", [128, 4096], "float32"),
     "kt": ("sbuf", [128, 4 * NP], "bfloat16"), "xt": ("sbuf", [128, 4 * NT], "bfloat16"), "nt": ("sbuf", [128, 4 * NT], "bfloat16"),
     "ut": ("sbuf", [128, 512], "bfloat16"), "vtile": ("sbuf", [128, 512], "bfloat16"),
-    "quc": ("sbuf", [128, 128], X4), "qus": ("sbuf", [128, 128], U8),
     "qvc": ("sbuf", [128, 128], X4), "qvs": ("sbuf", [128, 128], U8),
     "wqc": ("sbuf", [128, 512], X4), "wqs": ("sbuf", [128, 512], U8),
-    "zt": ("sbuf", [128, 1544], "bfloat16"), "ia": ("sbuf", [128, 128], "float32"), "ib": ("sbuf", [128, 128], "float32"),
+    "zt": ("sbuf", [128, 1544], "bfloat16"), "ib": ("sbuf", [128, 128], "float32"),
     "ec": ("sbuf", [128, 1536], X4), "es": ("sbuf", [128, 1536], U8),
-    "uli": ("sbuf", [128, 8], "int32"), "ul": ("sbuf", [128, 8], "uint16"),
-    "rr": ("sbuf", [128, 192], "float32"), "rt": ("sbuf", [128, 192], "float32"),
-    "cl": ("sbuf", [128, 8], "uint16"), "bias": ("sbuf", [128, 1], "float32"),
+    "rr": ("sbuf", [128, 64 + 96 * len(KINDS)], "float32"), "rt": ("sbuf", [128, 64 + 96 * len(KINDS)], "float32"),
+    "cl": ("sbuf", [128, 4 * len(KINDS)], "uint16"), "bias": ("sbuf", [128, 1], "float32"),
     "stw": ("sbuf", [128, 28], "int32"), "lst0": ("sbuf", [128, 140], "uint16"),
-    "lst1": ("sbuf", [128, 144], "uint16"), "lst2": ("sbuf", [128, 144], "uint16"),
-    "nxl": ("sbuf", [128, 80], "int32"), "nxa0": ("sbuf", [128, 80], "float32"),
+    "lst1": ("sbuf", [128, 48 * NC], "uint16"), "lst2": ("sbuf", [128, 48 * NC], "uint16"),
+    "nxl": ("sbuf", [128, 80], "int32"), "nxh": ("sbuf", [128, 80], "float32"), "nxa0": ("sbuf", [128, 80], "float32"),
     "nxa1": ("sbuf", [128, 80], "float32"), "nxa2": ("sbuf", [128, 80], "float32"),
-    "mm": ("sbuf", [128, 512], "float16"), "tt": ("sbuf", [128, 992], "float16"), "tl": ("sbuf", [128, NT], "float16"),
-    "zc": ("sbuf", [128, 192], "float32"), "zf": ("sbuf", [128, 32], "float32"), "zo": ("sbuf", [128, 32], "float32"),
+    "win0": ("sbuf", [128, NP], "float32"), "win1": ("sbuf", [128, NP], "float32"),
+    "mm": ("sbuf", [128, NT + 16 * NC + 16], "float16"), "tt": ("sbuf", [128, 2 * NT + 32 * NC], "float16"), "tl": ("sbuf", [128, NT], "float16"),
+    "zc": ("sbuf", [128, 80 * NC], "float32"), "zf": ("sbuf", [128, 32], "float32"), "zo": ("sbuf", [128, 32], "float32"),
     "ysb": ("sbuf", [128, NT], "float32"),
     "hc": ("sbuf", [128, HALF], X4), "hs": ("sbuf", [128, HALF], U8),
     "sc3": ("sbuf", [128, NT], X4), "ss3": ("sbuf", [128, NT], U8),
@@ -40,7 +39,6 @@ SCRATCH = {
 for _t in range(NH):
     SCRATCH["tc%d" % _t] = ("sbuf", [128, TW], X4)
     SCRATCH["ts%d" % _t] = ("sbuf", [128, TW], U8)
-    SCRATCH["win%d" % _t] = ("sbuf", [128, NP], "float32")
     SCRATCH["pc%d" % _t] = ("sbuf", [128, 2 * NT], X4)
     SCRATCH["pz%d" % _t] = ("sbuf", [128, 2 * NT], U8)
     SCRATCH["sc%d" % _t] = ("sbuf", [128, NT], X4)
@@ -59,70 +57,50 @@ def chunks():
     return [(sum(SIZES[:c]), n) for c, n in enumerate(SIZES)]
 
 
-def list_pieces():
-    pieces, col = [], {}
-    blk = 0
-    for n in sorted(set(SIZES), reverse=True):
-        nq, nb = n // 16, n // 32
-        k = (3 * nq + 15) // 16
-        col[n] = (blk, k)
-        j = 0
-        while j < 16 * k:
-            l = min(j // nq, 2)
-            if j % 16 == 0 and nq == 8:
-                pieces.append((blk + j // 16, 0, 16, 0, (0, 0) if l == 0 else (0, 1), nb, 1 if l == 0 else 0))
-                j += 16
-                continue
-            end = min(16 * (j // 16 + 1), (l + 1) * nq if l < 2 else 16 * k)
-            pieces.append((blk + j // 16, j % 16, end - j, j - l * nq, ((0, 0), (1, 1), (0, 1))[l], nb, None))
-            j = end
-        blk += k
-    return pieces, col, blk
-
-
 def make_ops(cnt):
     ops, CH = [], chunks()
     A, F = AluOpType, ActivationFunctionType
-    pieces, col, nblk = list_pieces()
-    ng = 4 + 2 * len(pieces)
 
-    def add(name, eng, cost, deps, fn, ext=(), bank=None, src=None):
-        ops.append({"name": name, "eng": eng, "cost": cost, "deps": list(deps), "fn": fn, "ext": list(ext), "bank": bank, "src": src})
+    def add(name, eng, cost, deps, fn, ext=(), bank=None):
+        ops.append({"name": name, "eng": eng, "cost": cost, "deps": list(deps), "fn": fn, "ext": list(ext), "bank": bank})
 
     def move(e, on, out, in_, f=None):
         if on == "V":
             return e.tensor_copy(out, in_) if f is None else e.tensor_scalar(out, in_, f, None, A.mult)
         return e.activation(out, in_, F.Copy) if f is None else e.activation(out, in_, F.Copy, scale=f)
 
-    add("mz0", "V", ("h", 516), [], lambda e, T, k, on: e.memset(T.zt[:, 0:516], 0.0))
-    add("mz1", "V", ("h", 1028), [], lambda e, T, k, on: e.memset(T.zt[:, 516:1544], 0.0))
-    add("df", "V", ("c", 128), ["mz0"], lambda e, T, k, on: e.tensor_scalar(T.zt[:, 3:515:4], T.ib[:], 0.0, None, A.is_equal), [("G", 1)])
-    add("de", "V", ("c", 128), ["mz1"], lambda e, T, k, on: e.tensor_scalar(T.zt[:, 519:1031:4], T.ia[:], 0.0, None, A.is_equal), [("G", 2)])
-    add("do", "V", ("c", 128), ["mz1"], lambda e, T, k, on: e.tensor_scalar(T.zt[:, 1031:1543:4], T.ia[:], 1000.0, None, A.is_equal), [("G", 2)])
+    add("mz", "V", ("h", 516), [], lambda e, T, k, on: e.memset(T.zt[:, 0:516], 0.0))
+    add("df", "V", ("c", 128), ["mz"], lambda e, T, k, on: e.tensor_scalar(T.zt[:, 3:515:4], T.ib[:], 0.0, None, A.is_equal), [("G", 1)])
+    add("ra", "V", ("c", 64), [], lambda e, T, k, on: e.transpose(T.rt[:, 0:64], T.rr[:, 0:64]), [("G", 3)])
+    add("de", "F", ("h", 512), ["df", "ra"], lambda e, T, k, on:
+        e.tensor_scalar(T.zt[:, 516:1028], T.zt[:, 0:512], T.rt[:, 32:33], 0.0, A.add, A.max) if on == "V" else
+        e.activation(T.zt[:, 516:1028], T.zt[:, 0:512], F.Relu, bias=T.rt[:, 32:33]))
+    add("do", "F", ("h", 516), ["df", "ra"], lambda e, T, k, on:
+        e.tensor_scalar(T.zt[:, 1028:1544], T.zt[:, 0:516], T.rt[:, 32:33], -1.0, A.mult, A.mult) if on == "V" else
+        e.activation(T.zt[:, 1028:1544], T.zt[:, 0:516], F.Abs, scale=T.rt[:, 32:33]))
     for b in range(4):
         add("e%d" % b, "V", ("q", 128), ["df"], lambda e, T, k, on, b=b: e.quantize_mx(T.ec[:, 128 * b:128 * b + 128], T.es[:, 128 * b:128 * b + 128], T.zt[:, 3 - b:515 - b]))
         add("f%d" % b, "V", ("q", 256), ["de", "do"], lambda e, T, k, on, b=b:
             e.quantize_mx(T.ec[:, 512 + 256 * b:768 + 256 * b], T.es[:, 512 + 256 * b:768 + 256 * b], T.zt[:, 519 - b:1543 - b]))
-    for t in range(NH):
-        add("wi%d" % t, "S", ("c", NP), ["de", "do"], lambda e, T, k, on, t=t: e.activation(T["win%d" % t][:], T.zt[:, 516:516 + NP], F.Copy))
-    add("mi", "V", ("h", 512), ["df"], lambda e, T, k, on: e.tensor_copy(T.mm[:], T.zt[:, 0:512]))
+    for t in range(2):
+        add("wi%d" % t, "F", ("c", NP), ["de"], lambda e, T, k, on, t=t: move(e, on, T["win%d" % t][:], T.zt[:, 0:NP]))
+    add("mi", "V", ("h", NT + 16 * NC + 16), ["df"], lambda e, T, k, on: e.tensor_copy(T.mm[:], T.zt[:, 0:NT + 16 * NC + 16]))
     add("zi", "V", ("c", 4), [], lambda e, T, k, on: e.memset(T.zf[:, 28:32], 0.0))
-    for b in range(2):
-        add("nx%d" % b, "V", ("c", 40), [], lambda e, T, k, on, b=b: e.tensor_copy(T.nxa0[:, 40 * b:40 * b + 40], T.nxl[:, b:80:2]), [("lnx", 16)])
+    add("bi", "V", ("c", 1), ["ra"], lambda e, T, k, on: e.tensor_scalar(T.bias[:], T.rt[:, 0:1], 0.5, -2 * TINY, A.subtract, A.mult))
+    add("rb", "V", ("c", 96 * len(KINDS)), [], lambda e, T, k, on: e.transpose(T.rt[:, 64:], T.rr[:, 64:]), [("G", 3 + 6 * len(KINDS))])
+    for i, n in enumerate(KINDS):
+        add("cl%d" % n, "V", ("c", 3), ["rb"], lambda e, T, k, on, i=i, n=n:
+            e.tensor_scalar(T.cl[:, 4 * i:4 * i + 3], T.rt[:, 64 + 96 * i:160 + 96 * i:32], float(n // 8 + 1), 0.0, A.min, A.max))
+    add("nh", "V", ("c", 80), [], lambda e, T, k, on: e.tensor_scalar(T.nxh[:], T.nxl[:], 0.5, None, A.mult), [("lnx", 16)])
+    add("nx0", "V", ("c", 80), ["nh"], lambda e, T, k, on: e.tensor_tensor(T.nxa0[:, 0:40], T.nxh[:, 1:80:2], T.nxh[:, 0:80:2], A.subtract))
+    add("nx1", "V", ("c", 80), ["nh"], lambda e, T, k, on: e.tensor_tensor(T.nxa0[:, 40:80], T.nxh[:, 1:80:2], T.nxh[:, 0:80:2], A.add))
     for b in range(4):
         add("s%d" % b, "V", ("c", 28), [], lambda e, T, k, on, b=b: e.tensor_scalar(T.lst0[:, 28 * b:28 * b + 28], T.stw[:], 4.0, float(b), A.mult, A.add), [("lst", 16)])
     add("sn", "V", ("c", 28), [], lambda e, T, k, on: e.tensor_copy(T.lst0[:, 112:140], T.stw[:]), [("lst", 16)])
     add("qa", "V", ("q", HALF), [], lambda e, T, k, on: e.quantize_mx(T.tc0[:, 0:HALF], T.ts0[:, 0:HALF], T.kt[:, 0:4 * HALF]), [("ka", 16)])
     add("qb", "V", ("q", NP - HALF), [], lambda e, T, k, on: e.quantize_mx(T.tc0[:, HALF:NP], T.ts0[:, HALF:NP], T.kt[:, 4 * HALF:4 * NP]), [("kb", 16)])
-    add("qu", "V", ("q", 128), [], lambda e, T, k, on: e.quantize_mx(T.quc[:], T.qus[:], T.ut[:]), [("lu", 16)])
+    add("qu", "V", ("q", 128), [], lambda e, T, k, on: e.quantize_mx(T.tc0[:, NP:TW], T.ts0[:, NP:TW], T.ut[:]), [("lu", 16)])
     add("qv", "V", ("q", 128), [], lambda e, T, k, on: e.quantize_mx(T.qvc[:], T.qvs[:], T.vtile[:]), [("lv", 16)])
-    add("ul", "V", ("c", 8), [], lambda e, T, k, on: e.tensor_copy(T.ul[:], T.uli[:]), [("G", 3)])
-    add("uc", "V", ("g", 128), ["qu", "ul"], lambda e, T, k, on: e.tensor_copy(T.tc0[:, NP:TW].bitcast(dt.uint32), T.quc[:].bitcast(dt.uint32).indirect(T.ul[:, 0:8])))
-    add("us", "F", ("g", 128), ["qu", "ul"], lambda e, T, k, on: move(e, on, T.ts0[:, NP:TW], T.qus[:].indirect(T.ul[:, 0:8])))
-    w = 32 * nblk
-    add("rt", "V", ("c", w + 32), [], lambda e, T, k, on: e.transpose(T.rt[:, 0:w + 32], T.rr[:, 0:w + 32]), [("G", ng)])
-    add("cl", "V", ("c", 4), ["rt"], lambda e, T, k, on: e.tensor_scalar(T.cl[:, 0:nblk], T.rt[:, 0:w:32], float(max(SIZES) // 8 + 1), None, A.min))
-    add("bi", "S", ("c", 1), ["rt"], lambda e, T, k, on: e.activation(T.bias[:], T.rt[:, w:w + 1], F.Copy, scale=-TINY))
     for c, (o, n) in enumerate(CH):
         add("qs0_%d" % c, "V", ("q", n), [], lambda e, T, k, on, o=o, n=n: e.quantize_mx(T.sc0[:, o:o + n], T.ss0[:, o:o + n], T.xt[:, 4 * o:4 * (o + n)]), [("x%d" % c, 16)])
 
@@ -140,59 +118,64 @@ def make_ops(cnt):
                     e.quantize_mx(T.pc0[:, o:o + n], T.pz0[:, o:o + n], T.nt[:, 4 * o:4 * (o + n)]))
                 pn, ndep, nat = ["qn%d" % c], ["sn"], 112 + q0
             else:
-                ndep, nat, l = ["cp%d_%d" % (t - 1, c)], 48 * c + 2 * nq, 48 * c
+                ndep, nat, l = ["cp%d_%d" % (t - 1, c)], 48 * c + 32, 48 * c + 16 - nq
                 add("pc" + s, "V", ("g", 2 * n), ndep, lambda e, T, k, on, o=o, n=n, l=l, tc=tc, pc=pc, ls=ls:
                     e.tensor_copy(T[pc][:, 2 * o:2 * (o + n)].bitcast(dt.uint32), T[tc][:, 0:NP].bitcast(dt.uint32).indirect(T[ls][:, l:l + n // 8])), tab)
                 add("pz" + s, "F", ("g", 2 * n), ndep, lambda e, T, k, on, o=o, n=n, l=l, ts=ts, pz=pz, ls=ls:
                     move(e, on, T[pz][:, 2 * o:2 * (o + n)], T[ts][:, 0:NP].indirect(T[ls][:, l:l + n // 8])), tab)
                 pn = ["pc" + s, "pz" + s]
             for b in range(4):
-                def blend(e, T, k, on, b=b, t=t, o=o, n=n, pc=pc, pz=pz):
+                bk = "%d_%s" % (b, s)
+
+                def state(e, T, k, on, b=b, t=t, o=o, n=n):
+                    return e.matmul_mx(T.ps[:, 512 * k:512 * k + n], T.ec[:, 128 * b:128 * b + 128], T.es[:, 128 * b:128 * b + 128],
+                                       T["sc%d" % t][:, o:o + n], T["ss%d" % t][:, o:o + n], on, not on)
+
+                def nodes(e, T, k, on, b=b, t=t, o=o, n=n, pc=pc, pz=pz):
                     out = T.ps[:, 512 * k:512 * k + n]
-                    eb = 128 * b
-                    e.matmul_mx(out, T.ec[:, eb:eb + 128], T.es[:, eb:eb + 128], T["sc%d" % t][:, o:o + n], T["ss%d" % t][:, o:o + n], True, False)
                     if t == 0:
-                        return e.matmul_mx(out, T.ec[:, eb:eb + 128], T.es[:, eb:eb + 128], T.pc0[:, o:o + n], T.pz0[:, o:o + n], False, True)
+                        return e.matmul_mx(out, T.ec[:, 128 * b:128 * b + 128], T.es[:, 128 * b:128 * b + 128], T.pc0[:, o:o + n], T.pz0[:, o:o + n], on, not on)
                     eb = 512 + 256 * b
-                    e.matmul_mx(out, T.ec[:, eb:eb + 128], T.es[:, eb:eb + 128], T[pc][:, 2 * o:2 * o + n], T[pz][:, 2 * o:2 * o + n], False, False)
-                    return e.matmul_mx(out, T.ec[:, eb + 128:eb + 256], T.es[:, eb + 128:eb + 256], T[pc][:, 2 * o + n:2 * o + 2 * n], T[pz][:, 2 * o + n:2 * o + 2 * n], False, True)
-                add("b%d_%s" % (b, s), "P", ("p3" if t else "p2", n), pn + ["qs" + s, "e%d" % b] + (["f%d" % b] if t else []), blend, bank=True)
-                add("cv%d_%s" % (b, s), "F", ("c", n), ["b%d_%s" % (b, s)], lambda e, T, k, on, b=b, t=t, o=o, n=n:
-                    move(e, on, T["bt%d" % t][:, 4 * o + b:4 * (o + n):4], T.ps[:, 512 * k:512 * k + n], 0.5), src="b%d_%s" % (b, s))
+                    e.matmul_mx(out, T.ec[:, eb:eb + 128], T.es[:, eb:eb + 128], T[pc][:, 2 * o:2 * o + n], T[pz][:, 2 * o:2 * o + n], on, False)
+                    return e.matmul_mx(out, T.ec[:, eb + 128:eb + 256], T.es[:, eb + 128:eb + 256], T[pc][:, 2 * o + n:2 * o + 2 * n], T[pz][:, 2 * o + n:2 * o + 2 * n], False, not on)
+                add("a" + bk, "P", ("p1", n), ["qs" + s, "e%d" % b], state, bank="b" + bk)
+                add("n" + bk, "P", ("p2" if t else "p1", n), pn + ["f%d" % b if t else "e%d" % b], nodes, bank="b" + bk)
+                add("cv" + bk, "F", ("c", n), ["a" + bk, "n" + bk], lambda e, T, k, on, b=b, t=t, o=o, n=n:
+                    move(e, on, T["bt%d" % t][:, 4 * o + b:4 * (o + n):4], T.ps[:, 512 * k:512 * k + n], 0.5), bank="b" + bk)
             add("qv" + s, "V", ("q", n), ["cv%d_%s" % (b, s) for b in range(4)], lambda e, T, k, on, t=t, o=o, n=n:
                 e.quantize_mx(T["vc%d" % t][:, o:o + n], T["vs%d" % t][:, o:o + n], T["bt%d" % t][:, 4 * o:4 * (o + n)]))
-            add("sc" + s, "P", ("p1", n), ["qv" + s] + (["uc", "us"] if t == 0 else []), lambda e, T, k, on, t=t, o=o, n=n, tc=tc, ts=ts:
-                e.matmul_mx(T.ps[:, 512 * k:512 * k + n], T[tc][:, NP:TW], T[ts][:, NP:TW], T["vc%d" % t][:, o:o + n], T["vs%d" % t][:, o:o + n], True, True), utab, bank=True)
+            add("sc" + s, "P", ("p1", n), ["qv" + s] + (["qu"] if t == 0 else []), lambda e, T, k, on, t=t, o=o, n=n, tc=tc, ts=ts:
+                e.matmul_mx(T.ps[:, 512 * k:512 * k + n], T[tc][:, NP:TW], T[ts][:, NP:TW], T["vc%d" % t][:, o:o + n], T["vs%d" % t][:, o:o + n], True, True), utab, "s" + s)
             for b in range(4):
-                add("l%d_%s" % (b, s), "P", ("p1", n), ["qv" + s], lambda e, T, k, on, b=b, t=t, o=o, n=n:
+                bk = "%d_%s" % (b, s)
+                add("l" + bk, "P", ("p1", n), ["qv" + s], lambda e, T, k, on, b=b, t=t, o=o, n=n:
                     e.matmul_mx(T.ps[:, 512 * k:512 * k + n], T.wqc[:, 128 * b:128 * b + 128], T.wqs[:, 128 * b:128 * b + 128], T["vc%d" % t][:, o:o + n], T["vs%d" % t][:, o:o + n], True, True),
-                    [("lw", 32)], bank=True)
-                add("cr%d_%s" % (b, s), "F", ("c", n), ["l%d_%s" % (b, s)], lambda e, T, k, on, b=b, t=t, o=o, n=n:
-                    move(e, on, T["lt%d" % t][:, 4 * o + b:4 * (o + n):4], T.ps[:, 512 * k:512 * k + n], 0.03125), src="l%d_%s" % (b, s))
+                    [("lw", 32)], "l" + bk)
+                add("cr" + bk, "F", ("c", n), ["l" + bk], lambda e, T, k, on, b=b, t=t, o=o, n=n:
+                    move(e, on, T["lt%d" % t][:, 4 * o + b:4 * (o + n):4], T.ps[:, 512 * k:512 * k + n], 0.03125), bank="l" + bk)
             add("qs%d_%d" % (t + 1, c), "V", ("q", n), ["cr%d_%s" % (b, s) for b in range(4)], lambda e, T, k, on, t=t, o=o, n=n:
                 e.quantize_mx(T["sc%d" % (t + 1)][:, o:o + n], T["ss%d" % (t + 1)][:, o:o + n], T["lt%d" % t][:, 4 * o:4 * (o + n)]))
             add("sg" + s, "S", ("c", n), ["sc" + s, "bi"], lambda e, T, k, on, t=t, o=o, n=n:
-                e.activation(T["sg%d" % t][:, o:o + n], T.ps[:, 512 * k:512 * k + n], F.Sign, bias=T.bias[:, 0:1], scale=T.rt[:, w:w + 1]), src="sc" + s)
+                e.activation(T["sg%d" % t][:, o:o + n], T.ps[:, 512 * k:512 * k + n], F.Sign, bias=T.bias[:, 0:1], scale=T.rt[:, 0:1]), bank="s" + s)
             m = o + 16 * (c + 1)
             add("mg" + s, "V", ("g", n), ["sg" + s, "mi"] + ndep, lambda e, T, k, on, t=t, o=o, n=n, m=m, ls=ls, nat=nat, nq=nq:
-                e.tensor_tensor(T.mm[:, m:m + n], T["win%d" % t][:].indirect(T[ls][:, nat:nat + nq]), T["sg%d" % t][:, o:o + n], A.mult), [("w%d" % t, 32)])
+                e.tensor_tensor(T.mm[:, m:m + n], T["win%d" % (t % 2)][:].indirect(T[ls][:, nat:nat + nq]), T["sg%d" % t][:, o:o + n], A.mult), [("w%d" % t, 32)])
             if t < NH - 1:
-                z, to = 96 * t + 32 * c, 2 * o + 32 * c
-                lc, lk = col[n]
+                z, to, lc = 40 * (NC * t + c), 2 * o + 32 * c, 4 * KINDS.index(n)
                 add("t1" + s, "V", ("h", n), ["mg" + s], lambda e, T, k, on, n=n, m=m, to=to: e.transpose(T.tt[:, to:to + n], T.mm[:, m:m + n]))
                 add("t2" + s, "V", ("h", n + 32), ["mg" + s], lambda e, T, k, on, n=n, m=m, to=to: e.transpose(T.tt[:, to + n:to + 2 * n + 32], T.mm[:, m - 16:m + n + 16]))
                 add("mx" + s, "V", ("c", 8 * nb + 4), ["t1" + s, "t2" + s], lambda e, T, k, on, n=n, to=to, z=z, nb=nb:
-                    e.tensor_tensor(T.zc[:, z:z + 4 * nb + 2], T.tt[:, to:to + 2 * n + 32:16], T.tt[:, to + 1:to + 2 * n + 32:16], A.max))
-                add("cp" + s, "V", ("g", 16 * lk), ["mx" + s, "cl"], lambda e, T, k, on, t=t, c=c, z=z, nb=nb, lc=lc, lk=lk:
-                    e.tensor_copy(T["lst%d" % (t + 1)][:, 48 * c:48 * c + 16 * lk], T.zc[:, z:z + 4 * nb + 2].indirect(T.cl[:, lc:lc + lk])))
+                    e.tensor_tensor(T.zc[:, z:z + 4 * nb + 2], T.tt[:, to:to + 2 * n + 32:16], T.tt[:, to + 1:to + 2 * n + 32:16], A.add))
+                add("cp" + s, "V", ("g", 48), ["mx" + s, "cl%d" % n], lambda e, T, k, on, t=t, c=c, z=z, nb=nb, lc=lc:
+                    e.tensor_copy(T["lst%d" % (t + 1)][:, 48 * c:48 * c + 48], T.zc[:, z:z + 4 * nb + 2].indirect(T.cl[:, lc:lc + 3])))
             else:
                 add("t1" + s, "V", ("h", n), ["mg" + s], lambda e, T, k, on, o=o, n=n, m=m: e.transpose(T.tl[:, o:o + n], T.mm[:, m:m + n]))
                 add("y%d" % c, "P", ("p1", n), ["qs3_%d" % c, "qv"], lambda e, T, k, on, o=o, n=n:
-                    e.matmul_mx(T.ps[:, 512 * k:512 * k + n], T.qvc[:], T.qvs[:], T.sc3[:, o:o + n], T.ss3[:, o:o + n], True, True), bank=True)
-                add("cy%d" % c, "F", ("c", n), ["y%d" % c], lambda e, T, k, on, o=o, n=n: move(e, on, T.ysb[:, o:o + n], T.ps[:, 512 * k:512 * k + n]), src="y%d" % c)
-    tl = ["t1%d_%d" % (NH - 1, c) for c in range(len(CH))]
+                    e.matmul_mx(T.ps[:, 512 * k:512 * k + n], T.qvc[:], T.qvs[:], T.sc3[:, o:o + n], T.ss3[:, o:o + n], True, True), bank="y%d" % c)
+                add("cy%d" % c, "F", ("c", n), ["y%d" % c], lambda e, T, k, on, o=o, n=n: move(e, on, T.ysb[:, o:o + n], T.ps[:, 512 * k:512 * k + n]), bank="y%d" % c)
+    tl = ["t1%d_%d" % (NH - 1, c) for c in range(NC)]
     for h in range(2):
-        add("fm%d" % h, "V", ("c", 28), tl, lambda e, T, k, on, h=h: e.tensor_tensor(T.zf[:, 14 * h:14 * h + 14], T.tl[:, 16 * h:NT:32], T.tl[:, 16 * h + 1:NT:32], A.max))
+        add("fm%d" % h, "V", ("c", 28), tl, lambda e, T, k, on, h=h: e.tensor_tensor(T.zf[:, 14 * h:14 * h + 14], T.tl[:, 16 * h:NT:32], T.tl[:, 16 * h + 1:NT:32], A.add))
     add("ft", "V", ("c", 32), ["fm0", "fm1", "zi"], lambda e, T, k, on: e.transpose(T.zo[:], T.zf[:]))
     return ops
 
@@ -238,8 +221,7 @@ def plan(T, topo):
         put(me, ("iota", 0))
         put(me, ("wait", ["qb"]))
         send(me, d1, "t0", "t1", HALF, NP, "k1", first)
-        put(me, ("iota", 1))
-        put(me, ("wait", ["uc", "us"]))
+        put(me, ("wait", ["qu"]))
         send(me, d1, "t0", "t1", NP, TW, "u1", first)
         put(me, ("sem", "k1"))
         if near:
@@ -255,12 +237,35 @@ def plan(T, topo):
 BUF = {"t0": ("tc0", "ts0"), "t1": ("tc1", "ts1"), "t2": ("tc2", "ts2"), "h": ("hc", "hs")}
 
 
-def list_rows(g, T, blk, j0, ln, q, hs, nb, rep):
-    for u in range(2):
-        base, step = (q + hs[u], 2 * nb + 2) if u == 0 else (2 * nb + q + hs[u], -2 * nb)
-        pat = [[2, ln // 2], [step, 2]] if rep is None else [[rep, 2], [2, ln // 4], [step, 2]]
-        a = 32 * blk + 16 * u + j0
-        g.iota(T.rr[:, a:a + ln], pat, base, 0, allow_small_or_imprecise_dtypes=True).then_inc(T.sem.G, 1)
+def list_rows():
+    rows = []
+    for i, n in enumerate(KINDS):
+        nb = n // 32
+        for l, (q, hs) in enumerate(((n // 16 - 16, (0, 0)), (0, (1, 1)), (0, (0, 1)))):
+            a = 64 + 96 * i + 32 * l
+            rows.append((a, [[2, 8], [2 * nb + 2, 2]], q + hs[0]))
+            rows.append((a + 16, [[2, 8], [-2 * nb, 2]], 2 * nb + q + hs[1]))
+    return rows
+
+
+def lay_out(ops, seq):
+    by = {o["name"]: o for o in ops}
+    order, bank, before, opens = {"P": [], "V": [], "S": []}, {}, {}, {}
+    free = [(k, None) for k in range(8)]
+    for x in seq:
+        n = x.rstrip("*")
+        o = by[n]
+        order[o["eng"] if o["eng"] != "F" else "V" if x != n else "S"].append(n)
+        r = o["bank"]
+        if r and o["eng"] == "P":
+            opens[n] = r not in bank
+            if opens[n]:
+                bank[r], last = free.pop(0)
+                if last:
+                    before[n] = last
+        elif r:
+            free.append((bank[r], n))
+    return order, bank, before, opens
 
 
 def waits(order, idx, by, before):
@@ -296,24 +301,18 @@ def rank_program(g, core, T, topo):
     rank = T.rank_of(core)
     sem, CH = T.sem, chunks()
     idx = {}
-    pieces, col, nblk = list_pieces()
-    late = pieces[4:]
+    rows = list_rows()
+
+    def iota(a, pat, base):
+        g.iota(T.rr[:, a:a + pat[0][1] * pat[1][1]], pat, base, 0, allow_small_or_imprecise_dtypes=True).then_inc(sem.G, 1)
+
     if rank is not None:
         ops = make_ops({s: got[(core, s)] for s in ("k1", "u1", "k2")})
         by = {o["name"]: o for o in ops}
-        order, bank, before = {}, {}, {}
-        for e in ORDER:
-            order[e] = [x.split(":")[0] for x in ORDER[e].split()]
+        order, bank, before, opens = lay_out(ops, ORDER.split())
+        for e in order:
             for i, n in enumerate(order[e]):
                 idx[n] = (e, i + 1)
-        reader = {o["src"]: o["name"] for o in ops if o["src"]}
-        last = {}
-        for x in ORDER["P"].split():
-            n, k = x.split(":")
-            bank[n] = bank[reader[n]] = int(k)
-            if k in last:
-                before[n] = last[k]
-            last[k] = reader[n]
         todo = waits(order, idx, by, before)
 
         def waiter(q):
@@ -325,51 +324,48 @@ def rank_program(g, core, T, topo):
                     seen[s] = v
             return need
 
+        def after(need, ds):
+            for e in order:
+                need(e, max([0] + [idx[d][1] for d in ds if idx[d][0] == e]))
+
         sy, sc = g.sync, g.scalar
         sc.dma_start(T.nxl[:], T.nx[:]).then_inc(sem.lnx, 16)
-        sy.dma_start(T.kt[:, 0:4 * HALF], T.k[:, 0:4 * HALF]).then_inc(sem.ka, 16)
-        sy.dma_start(T.kt[:, 4 * HALF:4 * NP], T.k[:, 4 * HALF:4 * NP]).then_inc(sem.kb, 16)
         sc.dma_start(T.stw[:], T.st[:]).then_inc(sem.lst, 16)
-        xs = [(T.xt[:, 4 * o:4 * (o + n)], T.x[:, 4 * o:4 * (o + n)]) for o, n in CH]
-        sy.dma_start(*xs[0]).then_inc(sem.x0, 16)
-        sy.dma_start(T.ut[:], T.u[:]).then_inc(sem.lu, 16)
-        sy.dma_start(*xs[1]).then_inc(sem.x1, 16)
-        sy.dma_start(T.wqc[:].bitcast(dt.uint8), T.wc[:]).then_inc(sem.lw, 16)
-        sy.dma_start(T.wqs[:], T.ws[:]).then_inc(sem.lw, 16)
-        if len(CH) > 2:
-            sy.dma_start(*xs[2]).then_inc(sem.x2, 16)
         ns = waiter(sy)
+        loads = {"ka": [(T.kt[:, 0:4 * HALF], T.k[:, 0:4 * HALF], "ka")], "kb": [(T.kt[:, 4 * HALF:4 * NP], T.k[:, 4 * HALF:4 * NP], "kb")],
+                 "u": [(T.ut[:], T.u[:], "lu")], "v": [(T.vtile[:], T.v[:], "lv")],
+                 "W": [(T.wqc[:].bitcast(dt.uint8), T.wc[:], "lw"), (T.wqs[:], T.ws[:], "lw")]}
+        for c, (o, n) in enumerate(CH):
+            loads["x%d" % c] = [(T.xt[:, 4 * o:4 * (o + n)], T.x[:, 4 * o:4 * (o + n)], "x%d" % c)]
         for t in range(NH):
-            ns(*idx["wi%d" % t])
-            if t == 0:
-                ns(*idx["nx0"])
-                ns(*idx["nx1"])
-            else:
-                ns("n%d" % t, got[(core, "n%d" % t)])
-            for b in range(2):
-                sy.dma_start(T["win%d" % t][b:128:16, :], T["nxa%d" % t][:, 40 * b:40 * b + 40]).then_inc(sem["w%d" % t], 16)
-        sy.dma_start(T.vtile[:], T.v[:]).then_inc(sem.lv, 16)
+            loads["w%d" % t] = [(T["win%d" % (t % 2)][b:128:16, :], T["nxa%d" % t][:, 40 * b:40 * b + 40], "w%d" % t) for b in range(2)]
+        for x in LOADS.split():
+            if x in ("w0", "w1", "w2"):
+                after(ns, {"w0": ["wi0", "nx0", "nx1"], "w1": ["wi1"], "w2": ["mg0_%d" % c for c in range(NC)]}[x])
+                if x != "w0":
+                    ns("n" + x[1], got[(core, "n" + x[1])])
+            for dst, src, s in loads[x]:
+                sy.dma_start(dst, src).then_inc(sem[s], 16)
 
         stores = {}
         for c, (o, n) in enumerate(CH):
             stores["oc%d" % c] = (["qs3_%d" % c], T.oc[:, 4 * o:4 * (o + n)], T.sc3[:, o:o + n].bitcast(dt.uint8))
             stores["y%d" % c] = (["cy%d" % c], T.y[:, o:o + n], T.ysb[:, o:o + n])
         for a in range(4):
-            stores["os%d" % a] = (["qs3_%d" % c for c in range(len(CH))], T.osc[4 * a:4 * a + 4, :], T.ss3[32 * a:32 * a + 4, :])
+            stores["os%d" % a] = (["qs3_%d" % c for c in range(NC)], T.osc[4 * a:4 * a + 4, :], T.ss3[32 * a:32 * a + 4, :])
             stores["pl%d" % a] = (["ft"], T.pl[2 * a:2 * a + 2, :], T.zo[32 * a:32 * a + 28, :])
 
         def store(q, need, names):
             for x in names.split():
                 ds, dst, src = stores[x]
-                for e in order:
-                    need(e, max([0] + [idx[d][1] for d in ds if idx[d][0] == e]))
+                after(need, ds)
                 q.dma_start(dst, src).then_inc(sem.out, 16)
 
         for e, q in (("P", g.tensor), ("V", g.vector), ("S", g.scalar)):
             for n in order[e]:
                 for s, v in todo[n].items():
                     q.wait_ge(sem[s], v)
-                by[n]["fn"](q, T, bank.get(n), e).then_inc(sem[e], 1)
+                by[n]["fn"](q, T, bank.get(by[n]["bank"]), opens[n] if e == "P" else e).then_inc(sem[e], 1)
             if e == "S":
                 store(q, waiter(q), STORES[1])
         store(sy, ns, STORES[0])
@@ -377,13 +373,11 @@ def rank_program(g, core, T, topo):
             ns(e, len(order[e]))
         ns("out", 16 * len(stores))
 
-        flag = {"allow_small_or_imprecise_dtypes": True}
-        g.iota(T.ib[:], [[-1, 128]], 0, 1, **flag).then_inc(sem.G, 1)
-        g.iota(T.ia[:], [[-32, 4], [984, 2], [-1, 16]], 0, 1, **flag).then_inc(sem.G, 1)
-        g.iota(T.uli[:], [[16, 8]], 0, 0).then_inc(sem.G, 1)
-        g.iota(T.rr[:, 32 * nblk:32 * nblk + 32], [[0, 16], [2, 2]], -1, 0, **flag).then_inc(sem.G, 1)
-        for p in pieces[:4]:
-            list_rows(g, T, *p)
+        g.iota(T.ib[:], [[-1, 128]], 0, 1, allow_small_or_imprecise_dtypes=True).then_inc(sem.G, 1)
+        iota(0, [[0, 2], [-1, 16]], 1)
+        iota(32, [[-1, 2], [0, 16]], 0)
+        for p in rows[:EARLY]:
+            iota(*p)
 
     for it in calls.get(core, []):
         if it[0] == "nx":
@@ -399,8 +393,8 @@ def rank_program(g, core, T, topo):
         elif it[0] == "sem":
             g.wait_ge(sem[it[1]], got[(core, it[1])])
         elif it[0] == "iota":
-            for p in late[it[1]::2]:
-                list_rows(g, T, *p)
+            for p in rows[EARLY:]:
+                iota(*p)
         else:
             x, d, kind, a, b, c0, c1, s, eng = it
             rid, pid, se = topo.addr(d)

@@ -1,17 +1,19 @@
+import math
 from concourse.bass import DstId, RemoteDMATransfer
 from concourse.mybir import dt, AluOpType, ActivationFunctionType
 
 NT, NP, NH = 448, 640, 3
 SIZES = [160, 160, 128]
-HALF = 320
-CUT = 448
+HALF = 448
 TW = NP + 128
 TINY = 2.0 ** -120
 X4, U8 = "float8_e4m3fn_x4", "uint8"
-ORDER = "mz df ra do zi e0 de* e3 f3 wi1 wi0 nh s0 s3 nx1 nx0 s2 e1 s1 e2 qa f2 f0 f1 g0_0 g1_0 g2_0 g3_0* qb qs0_0 qn0 rb g0_1* g2_1 g3_1 g1_1 a3_0_0 a2_0_0 qs0_1 n3_0_0 cv3_0_0 n2_0_0 a0_0_0 n0_0_0 n1_0_0 a1_0_0 cv2_0_0 cv0_0_0 cv1_0_0 cl160 qn1 a1_0_1 n1_0_1 a0_0_1 g2_2 g3_2 cv1_0_1 qu g0_2* mi n0_0_1 a2_0_1 n2_0_1 n3_0_1 a3_0_1 cv2_0_1 qv0_0 sc0_0 g1_2* bi sn qs0_2 qn2 cv0_0_1* sg0_0 cv3_0_1 l3_0_0 l2_0_0 cr2_0_0* l0_0_0 a0_0_2 l1_0_0 n0_0_2 a3_0_2 n1_0_2 a2_0_2 a1_0_2 cr0_0_0 cr1_0_0 cr3_0_0 n2_0_2 n3_0_2 cv0_0_2 cv1_0_2 cv2_0_2 mg0_0 qv0_1 t20_0 t10_0 qs1_0 mx0_0 cv3_0_2* cp0_0 cl128 sc0_1 l3_0_1 sg0_1 qv0_2 cr3_0_1 l1_0_1 l0_0_1 pz1_0 mg0_1 pc1_0 t10_1 t20_1 a1_1_0 l2_0_1 cr2_0_1 a3_1_0 sc0_2 sg0_2 cr0_0_1 l0_0_2 l3_0_2 n2_1_0 n3_1_0 cr1_0_1 a0_1_0 n1_1_0 n0_1_0 a2_1_0 l1_0_2 cr3_0_2* mx0_1 mg0_2 cr0_0_2 cp0_1 qs1_1 cv3_1_0 t10_2 t20_2 pc1_1 mx0_2 cv1_1_0* pz1_1 cp0_2 a3_1_1 l2_0_2 a1_1_1 a2_1_1 cv2_1_0 cv0_1_0 qv1_0 cr2_0_2 cr1_0_2 pz1_2 n3_1_1 n1_1_1 a0_1_1 sc1_0 pc1_2 cv3_1_1* qs1_2 sg1_0 l0_1_0 n0_1_1 l1_1_0 l3_1_0 cr0_1_0 l2_1_0 n2_1_1 a0_1_2 a3_1_2 cr1_1_0 cv0_1_1 cv1_1_1 mg1_0 cr2_1_0 cr3_1_0* t11_0 t21_0 cv2_1_1* mx1_0 qv1_1 cp1_0 qs2_0 a1_1_2 n3_1_2 cv3_1_2 n0_1_2 cv0_1_2 n1_1_2 a2_1_2 n2_1_2 pc2_0 cv1_1_2 pz2_0 cv2_1_2* qv qv1_2 sc1_1 l3_1_1 l2_1_1 l1_1_1 a1_2_0 l0_1_1 n3_2_0 a3_2_0 sg1_1 cr2_1_1 cr1_1_1 cr0_1_1 n1_2_0 cv3_2_0 sc1_2 l2_1_2 l0_1_2 a2_2_0 n2_2_0 l3_1_2 cr2_1_2 sg1_2 cv1_2_0 mg1_1 cr3_1_1* t11_1 t21_1 qs2_1 mx1_1 cp1_1 mg1_2 cv2_2_0 pz2_1 a1_2_1 a0_2_0 a3_2_1 n0_2_0 l1_1_2 a2_2_1 a0_2_1 pc2_1 t21_2 t11_2 cr0_1_2* mx1_2 cv0_2_0 qv2_0 cp1_2 n1_2_1 n3_2_1 n2_2_1 cr3_1_2 cr1_1_2 qs2_2 cv1_2_1* pc2_2 cv3_2_1 pz2_2 l3_2_0 l0_2_0 n0_2_1 l2_2_0 a3_2_2 sc2_0 cr3_2_0* cv2_2_1 cv0_2_1 cr2_2_0* cr0_2_0* sg2_0 a2_2_2 n2_2_2 l1_2_0 a0_2_2 qv2_1 cv2_2_2 mg2_0 cr1_2_0 n1_2_2 n3_2_2 a1_2_2 n0_2_2 cv1_2_2 qs3_0 cv3_2_2* t12_0 cv0_2_2 l0_2_1 cr0_2_1* qv2_2 sc2_1 sg2_1 l1_2_1 l3_2_1 cr3_2_1* mg2_1 l2_2_1 cr1_2_1 cr2_2_1 sc2_2 l3_2_2 sg2_2 l0_2_2 l1_2_2 l2_2_2 y0 qs3_1 cr0_2_2* mg2_2 t12_1 cr3_2_2 cr1_2_2 cr2_2_2 qs3_2 y1 t12_2 fm1 fm0 y2 cy2* cy1 ft cy0"
-LOADS = "ka kb x0 u x1 W x2 w0 w1 v w2"
-STORES = ["oc0 oc1 y1 oc2 os1 os3 y2 pl1 pl3", "y0 os0 os2 pl0 pl2"]
-EARLY = 12
+ORDER = "mz df e1 wi0 ra mi nh de do e3 e2 nx0 nx1 s3 s1 s0 qa s2 qb g1_0 g0_0 g2_0 qu g3_0* g0_1 g2_1 g3_1 qs0_0 e0 qn0 a3_0_0 a0_0_0 a1_0_0 n3_0_0 qs0_1 sn bi g1_1* f0 n2_0_0 a2_0_0 a2_0_1 n1_0_0 n0_0_0 cv3_0_0 cv2_0_0 qn1 f3 qn2 cv1_0_0 cv0_0_0 a0_0_1 a3_0_1 a1_0_1 qs0_2 n3_0_1 n1_0_1 qv0_0 cv3_0_1 cv1_0_1 rb f2 n0_0_1 n2_0_1 n2_0_2 cv0_0_1 cv2_0_1 n3_0_2 sc0_0 a2_0_2 cl160 f1 cl128 sg0_0 qv0_1 a3_0_2 n0_0_2 a1_0_2 n1_0_2 a0_0_2 l2_0_0 cv2_0_2 cv3_0_2 cv1_0_2 mg0_0 l0_0_0 cr2_0_0* sc0_1 cv0_0_2 l3_0_0 cr0_0_0 t20_0 t10_0 l1_0_0 l3_0_1 qv0_2 sg0_1 l1_0_1 cr1_0_0* cr3_0_0 l2_0_1 l0_0_1 mx0_0 cr3_0_1 mg0_1 l1_0_2 sc0_2 l3_0_2 l2_0_2 cr1_0_1 cp0_0 cr2_0_1 cr0_0_1 qs1_0 t10_1 t20_1 sg0_2 pc1_0 pz1_0 a2_1_0 a3_1_0 l0_0_2 cr0_0_2 cr3_0_2 a1_1_0 a0_1_0 mx0_1 mg0_2 n3_1_0 n1_1_0 n2_1_0 cp0_1 cr2_0_2 cr1_0_2 qs1_1 t10_2 t20_2 pc1_1 pz1_1 mx0_2 n0_1_0 a1_1_1 a0_1_1 a2_1_1 a3_1_1 cv2_1_0* cv1_1_0* cv3_1_0 cv0_1_0 cp0_2 qs1_2 qv1_0 pc1_2 n3_1_1 cv3_1_1 pz1_2 n1_1_1 cv1_1_1* n2_1_1 n0_1_1 cv0_1_1* sc1_0 cv2_1_1 a1_1_2 l0_1_0 cr0_1_0* l2_1_0 l1_1_0 sg1_0 n1_1_2 qv1_1 cr2_1_0 a2_1_2 l3_1_0 n2_1_2 mg1_0 cr1_1_0 cr3_1_0 cv1_1_2 n0_1_2 cv2_1_2* sc1_1 sg1_1 t21_0 t11_0 l3_1_1 a0_1_2 qs2_0 n3_1_2 cr3_1_1 cv0_1_2* a3_1_2 mx1_0 l2_1_1 mg1_1 l1_1_1 cv3_1_2 l0_1_1 a3_2_0 a0_2_0 a1_2_0 cr2_1_1 cp1_0 qv1_2 cr1_1_1 t21_1 t11_1 cr0_1_1 pc2_0 pz2_0 a2_2_0 l2_1_2 sc1_2 sg1_2 l3_1_2 l1_1_2 mx1_1 qs2_1 cp1_1 mg1_2 n0_2_0 cr3_1_2 cr2_1_2 cr1_1_2 pc2_1 pz2_1 t11_2 t21_2 cv0_2_0* l0_1_2 n2_2_0 n3_2_0 a2_2_1 n1_2_0 a1_2_1 mx1_2 cr0_1_2 cv3_2_0 n2_2_1 cv2_2_0 cv1_2_0* n1_2_1 cp1_2 cv2_2_1 qs2_2 a0_2_1 n0_2_1 n3_2_1 a3_2_1 qv2_0 cv1_2_1 pc2_2 pz2_2 cv3_2_1* a3_2_2 a1_2_2 qv cv0_2_1 qv2_1 sc2_0 sg2_0 mg2_0 l0_2_0 a2_2_2 a0_2_2 cr0_2_0 n2_2_2 n0_2_2 cv2_2_2 cv0_2_2 n3_2_2 cv3_2_2* n1_2_2 l3_2_1 cr3_2_1 l3_2_0 cv1_2_2* l1_2_0 cr3_2_0* l2_2_1 l2_2_0 cr1_2_0 qv2_2 l0_2_1 cr2_2_1 l1_2_1 cr2_2_0* sc2_1 cr0_2_1 sc2_2 cr1_2_1* sg2_1 qs3_0 l3_2_2 l2_2_2 sg2_2 qs3_1 l1_2_2 l0_2_2 cr2_2_2 cr3_2_2* mg2_1 mg2_2 cr1_2_2 cr0_2_2 qs3_2 y0 cy0 y1 t12_0 t12_1 t12_2 fm1 fm0 ft cy1"
+LOADS = "ka kb u x0 x1 W x2 w0 w1 v w2"
+GSEG = [[0], [1, 2]]
+YSEG = [[0, 1], [2]]
+STORES = ["oc0 y0 oc1 os1 os3 y1 pl1 pl3", "os0 os2 pl0 pl2"]
+REL = HALF // 2
 KINDS = sorted(set(SIZES), reverse=True)
 NC = len(SIZES)
 
@@ -21,44 +23,40 @@ SCRATCH = {
     "ut": ("sbuf", [128, 512], "bfloat16"), "vtile": ("sbuf", [128, 512], "bfloat16"),
     "qvc": ("sbuf", [128, 128], X4), "qvs": ("sbuf", [128, 128], U8),
     "wqc": ("sbuf", [128, 512], X4), "wqs": ("sbuf", [128, 512], U8),
-    "zt": ("sbuf", [128, 1544], "bfloat16"), "ib": ("sbuf", [128, 128], "float32"),
+    "zt": ("sbuf", [128, 1672], "bfloat16"), "ib": ("sbuf", [128, 128], "float32"),
     "ec": ("sbuf", [128, 1536], X4), "es": ("sbuf", [128, 1536], U8),
-    "rr": ("sbuf", [128, 64 + 96 * len(KINDS)], "float32"), "rt": ("sbuf", [128, 64 + 96 * len(KINDS)], "float32"),
-    "cl": ("sbuf", [128, 4 * len(KINDS)], "uint16"), "bias": ("sbuf", [128, 1], "float32"),
+    "rr": ("sbuf", [128, 64 + 64 * len(KINDS)], "float32"), "rt": ("sbuf", [128, 64 + 64 * len(KINDS)], "float32"),
+    "cl": ("sbuf", [128, 2 * len(KINDS)], "uint16"), "bias": ("sbuf", [128, 1], "float32"),
     "stw": ("sbuf", [128, 28], "int32"), "lst0": ("sbuf", [128, 140], "uint16"),
-    "lst1": ("sbuf", [128, 48 * NC], "uint16"), "lst2": ("sbuf", [128, 48 * NC], "uint16"),
+    "lst1": ("sbuf", [128, 32 * NC], "uint16"), "lst2": ("sbuf", [128, 32 * NC], "uint16"),
     "nxl": ("sbuf", [128, 80], "int32"), "nxh": ("sbuf", [128, 80], "float32"), "nxa0": ("sbuf", [128, 80], "float32"),
     "nxa1": ("sbuf", [128, 80], "float32"), "nxa2": ("sbuf", [128, 80], "float32"),
     "win0": ("sbuf", [128, NP], "float32"), "win1": ("sbuf", [128, NP], "float32"),
     "mm": ("sbuf", [128, NT + 16 * NC + 16], "float16"), "tt": ("sbuf", [128, 2 * NT + 32 * NC], "float16"), "tl": ("sbuf", [128, NT], "float16"),
-    "zc": ("sbuf", [128, 80 * NC], "float32"), "zf": ("sbuf", [128, 32], "float32"), "zo": ("sbuf", [128, 32], "float32"),
-    "ysb": ("sbuf", [128, NT], "float32"),
-    "hc": ("sbuf", [128, HALF], X4), "hs": ("sbuf", [128, HALF], U8),
-    "sc3": ("sbuf", [128, NT], X4), "ss3": ("sbuf", [128, NT], U8),
+    "zc": ("sbuf", [128, 80 * NC], "float32"), "zo": ("sbuf", [128, 32], "float32"),
+    "ysb": ("sbuf", [128, NT], "float32"), "tch": ("sbuf", [128, HALF], X4),
+    "sc": ("sbuf", [128, (NH + 1) * NT], X4), "ss": ("sbuf", [128, (NH + 1) * NT], U8),
+    "vc": ("sbuf", [128, NH * NT], X4), "vs": ("sbuf", [128, NH * NT], U8),
+    "lt": ("sbuf", [128, 4 * NH * NT], "bfloat16"), "ml": ("sbuf", [128, NT], "float16"),
 }
 for _t in range(NH):
     SCRATCH["tc%d" % _t] = ("sbuf", [128, TW], X4)
     SCRATCH["ts%d" % _t] = ("sbuf", [128, TW], U8)
     SCRATCH["pc%d" % _t] = ("sbuf", [128, 2 * NT], X4)
     SCRATCH["pz%d" % _t] = ("sbuf", [128, 2 * NT], U8)
-    SCRATCH["sc%d" % _t] = ("sbuf", [128, NT], X4)
-    SCRATCH["ss%d" % _t] = ("sbuf", [128, NT], U8)
-    SCRATCH["vc%d" % _t] = ("sbuf", [128, NT], X4)
-    SCRATCH["vs%d" % _t] = ("sbuf", [128, NT], U8)
     SCRATCH["bt%d" % _t] = ("sbuf", [128, 4 * NT], "bfloat16")
-    SCRATCH["lt%d" % _t] = ("sbuf", [128, 4 * NT], "bfloat16")
     SCRATCH["sg%d" % _t] = ("sbuf", [128, NT], "bfloat16")
 
 SEMAPHORES = ["P", "V", "S", "G", "ka", "kb", "x0", "x1", "x2", "lu", "lw", "lv", "lst", "lnx", "w0", "w1", "w2",
-              "k1", "u1", "k2", "n1", "n2", "hcod", "hsca", "sent", "out"]
+              "hr", "ka1", "kr1", "kb1", "u1", "k2", "u2", "n1", "n2", "sent", "out"]
 
 
-def chunks():
-    return [(sum(SIZES[:c]), n) for c, n in enumerate(SIZES)]
+def span(cs):
+    return sum(SIZES[:cs[0]]), sum(SIZES[c] for c in cs)
 
 
 def make_ops(cnt):
-    ops, CH = [], chunks()
+    ops = []
     A, F = AluOpType, ActivationFunctionType
 
     def add(name, eng, cost, deps, fn, ext=(), bank=None):
@@ -69,28 +67,26 @@ def make_ops(cnt):
             return e.tensor_copy(out, in_) if f is None else e.tensor_scalar(out, in_, f, None, A.mult)
         return e.activation(out, in_, F.Copy) if f is None else e.activation(out, in_, F.Copy, scale=f)
 
-    add("mz", "V", ("h", 516), [], lambda e, T, k, on: e.memset(T.zt[:, 0:516], 0.0))
+    add("mz", "V", ("h", 644), [], lambda e, T, k, on: e.memset(T.zt[:, 0:644], 0.0))
     add("df", "V", ("c", 128), ["mz"], lambda e, T, k, on: e.tensor_scalar(T.zt[:, 3:515:4], T.ib[:], 0.0, None, A.is_equal), [("G", 1)])
+    add("mi", "V", ("h", NT + 16 * NC + 16), ["df"], lambda e, T, k, on: e.tensor_copy(T.mm[:], T.zt[:, 0:NT + 16 * NC + 16]))
     add("ra", "V", ("c", 64), [], lambda e, T, k, on: e.transpose(T.rt[:, 0:64], T.rr[:, 0:64]), [("G", 3)])
     add("de", "F", ("h", 512), ["df", "ra"], lambda e, T, k, on:
-        e.tensor_scalar(T.zt[:, 516:1028], T.zt[:, 0:512], T.rt[:, 32:33], 0.0, A.add, A.max) if on == "V" else
-        e.activation(T.zt[:, 516:1028], T.zt[:, 0:512], F.Relu, bias=T.rt[:, 32:33]))
+        e.tensor_scalar(T.zt[:, 644:1156], T.zt[:, 0:512], T.rt[:, 32:33], 0.0, A.add, A.max) if on == "V" else
+        e.activation(T.zt[:, 644:1156], T.zt[:, 0:512], F.Relu, bias=T.rt[:, 32:33]))
     add("do", "F", ("h", 516), ["df", "ra"], lambda e, T, k, on:
-        e.tensor_scalar(T.zt[:, 1028:1544], T.zt[:, 0:516], T.rt[:, 32:33], -1.0, A.mult, A.mult) if on == "V" else
-        e.activation(T.zt[:, 1028:1544], T.zt[:, 0:516], F.Abs, scale=T.rt[:, 32:33]))
+        e.tensor_scalar(T.zt[:, 1156:1672], T.zt[:, 0:516], T.rt[:, 32:33], -1.0, A.mult, A.mult) if on == "V" else
+        e.activation(T.zt[:, 1156:1672], T.zt[:, 0:516], F.Abs, scale=T.rt[:, 32:33]))
     for b in range(4):
         add("e%d" % b, "V", ("q", 128), ["df"], lambda e, T, k, on, b=b: e.quantize_mx(T.ec[:, 128 * b:128 * b + 128], T.es[:, 128 * b:128 * b + 128], T.zt[:, 3 - b:515 - b]))
         add("f%d" % b, "V", ("q", 256), ["de", "do"], lambda e, T, k, on, b=b:
-            e.quantize_mx(T.ec[:, 512 + 256 * b:768 + 256 * b], T.es[:, 512 + 256 * b:768 + 256 * b], T.zt[:, 519 - b:1543 - b]))
-    for t in range(2):
-        add("wi%d" % t, "F", ("c", NP), ["de"], lambda e, T, k, on, t=t: move(e, on, T["win%d" % t][:], T.zt[:, 0:NP]))
-    add("mi", "V", ("h", NT + 16 * NC + 16), ["df"], lambda e, T, k, on: e.tensor_copy(T.mm[:], T.zt[:, 0:NT + 16 * NC + 16]))
-    add("zi", "V", ("c", 4), [], lambda e, T, k, on: e.memset(T.zf[:, 28:32], 0.0))
+            e.quantize_mx(T.ec[:, 512 + 256 * b:768 + 256 * b], T.es[:, 512 + 256 * b:768 + 256 * b], T.zt[:, 647 - b:1671 - b]))
+    add("wi0", "F", ("c", NP), ["df"], lambda e, T, k, on: move(e, on, T.win0[:], T.zt[:, 0:NP]))
     add("bi", "V", ("c", 1), ["ra"], lambda e, T, k, on: e.tensor_scalar(T.bias[:], T.rt[:, 0:1], 0.5, -2 * TINY, A.subtract, A.mult))
-    add("rb", "V", ("c", 96 * len(KINDS)), [], lambda e, T, k, on: e.transpose(T.rt[:, 64:], T.rr[:, 64:]), [("G", 3 + 6 * len(KINDS))])
+    add("rb", "V", ("c", 64 * len(KINDS)), [], lambda e, T, k, on: e.transpose(T.rt[:, 64:], T.rr[:, 64:]), [("G", 3 + len(list_rows()))])
     for i, n in enumerate(KINDS):
-        add("cl%d" % n, "V", ("c", 3), ["rb"], lambda e, T, k, on, i=i, n=n:
-            e.tensor_scalar(T.cl[:, 4 * i:4 * i + 3], T.rt[:, 64 + 96 * i:160 + 96 * i:32], float(n // 8 + 1), 0.0, A.min, A.max))
+        add("cl%d" % n, "V", ("c", 2), ["rb"], lambda e, T, k, on, i=i, n=n:
+            e.tensor_scalar(T.cl[:, 2 * i:2 * i + 2], T.rt[:, 64 + 64 * i:128 + 64 * i:32], float(n // 8 + 1), 0.0, A.min, A.max))
     add("nh", "V", ("c", 80), [], lambda e, T, k, on: e.tensor_scalar(T.nxh[:], T.nxl[:], 0.5, None, A.mult), [("lnx", 16)])
     add("nx0", "V", ("c", 80), ["nh"], lambda e, T, k, on: e.tensor_tensor(T.nxa0[:, 0:40], T.nxh[:, 1:80:2], T.nxh[:, 0:80:2], A.subtract))
     add("nx1", "V", ("c", 80), ["nh"], lambda e, T, k, on: e.tensor_tensor(T.nxa0[:, 40:80], T.nxh[:, 1:80:2], T.nxh[:, 0:80:2], A.add))
@@ -101,35 +97,38 @@ def make_ops(cnt):
     add("qb", "V", ("q", NP - HALF), [], lambda e, T, k, on: e.quantize_mx(T.tc0[:, HALF:NP], T.ts0[:, HALF:NP], T.kt[:, 4 * HALF:4 * NP]), [("kb", 16)])
     add("qu", "V", ("q", 128), [], lambda e, T, k, on: e.quantize_mx(T.tc0[:, NP:TW], T.ts0[:, NP:TW], T.ut[:]), [("lu", 16)])
     add("qv", "V", ("q", 128), [], lambda e, T, k, on: e.quantize_mx(T.qvc[:], T.qvs[:], T.vtile[:]), [("lv", 16)])
-    for c, (o, n) in enumerate(CH):
-        add("qs0_%d" % c, "V", ("q", n), [], lambda e, T, k, on, o=o, n=n: e.quantize_mx(T.sc0[:, o:o + n], T.ss0[:, o:o + n], T.xt[:, 4 * o:4 * (o + n)]), [("x%d" % c, 16)])
+    for c in range(NC):
+        o, n = span([c])
+        add("qs0_%d" % c, "V", ("q", n), [], lambda e, T, k, on, o=o, n=n: e.quantize_mx(T.sc[:, o:o + n], T.ss[:, o:o + n], T.xt[:, 4 * o:4 * (o + n)]), [("x%d" % c, 16)])
+    for cs in GSEG:
+        o, n = span(cs)
+        for b in range(4):
+            add("g%d_%d" % (b, cs[0]), "F", ("g", n), ["s%d" % b], lambda e, T, k, on, b=b, o=o, n=n:
+                move(e, on, T.nt[:, 4 * o + b:4 * (o + n):4], T.kt[:].indirect(T.lst0[:, 28 * b + o // 16:28 * b + (o + n) // 16])), [("ka", 16), ("kb", 16)])
 
     for t in range(NH):
-        tab = {0: [], 1: [("k1", cnt["k1"])], 2: [("k2", cnt["k2"])]}[t]
-        utab = {0: [], 1: [("u1", cnt["u1"])], 2: tab}[t]
-        for c, (o, n) in enumerate(CH):
-            s, nq, q0, nb = "%d_%d" % (t, c), n // 16, o // 16, n // 32
-            tc, ts, pc, pz, ls = "tc%d" % t, "ts%d" % t, "pc%d" % t, "pz%d" % t, "lst%d" % t
+        tab = [(s, cnt[s]) for s in ([], ["ka1", "kr1", "kb1"], ["k2"])[t]]
+        utab = tab + [(s, cnt[s]) for s in ([], ["u1"], ["u2"])[t]]
+        tc, ts, pc, pz, ls = "tc%d" % t, "ts%d" % t, "pc%d" % t, "pz%d" % t, "lst%d" % t
+        for c in range(NC):
+            o, n = span([c])
+            s, nq, nb, h = "%d_%d" % (t, c), n // 16, n // 32, NT * t + o
             if t == 0:
-                for b in range(4):
-                    add("g%d_%d" % (b, c), "F", ("g", n), ["s%d" % b], lambda e, T, k, on, b=b, o=o, n=n, q0=q0, nq=nq:
-                        move(e, on, T.nt[:, 4 * o + b:4 * (o + n):4], T.kt[:].indirect(T.lst0[:, 28 * b + q0:28 * b + q0 + nq])), [("ka", 16), ("kb", 16)])
-                add("qn%d" % c, "V", ("q", n), ["g%d_%d" % (b, c) for b in range(4)], lambda e, T, k, on, o=o, n=n:
+                add("qn%d" % c, "V", ("q", n), ["g%d_%d" % (b, cs[0]) for b in range(4) for cs in GSEG if c in cs], lambda e, T, k, on, o=o, n=n:
                     e.quantize_mx(T.pc0[:, o:o + n], T.pz0[:, o:o + n], T.nt[:, 4 * o:4 * (o + n)]))
-                pn, ndep, nat = ["qn%d" % c], ["sn"], 112 + q0
+                pn, ndep, nat = ["qn%d" % c], ["sn"], 112 + o // 16
             else:
-                ndep, nat, l = ["cp%d_%d" % (t - 1, c)], 48 * c + 32, 48 * c + 16 - nq
+                pn, ndep, nat, l = ["pc" + s, "pz" + s], ["cp%d_%d" % (t - 1, c)], 32 * c + 2 * nq, 32 * c
                 add("pc" + s, "V", ("g", 2 * n), ndep, lambda e, T, k, on, o=o, n=n, l=l, tc=tc, pc=pc, ls=ls:
                     e.tensor_copy(T[pc][:, 2 * o:2 * (o + n)].bitcast(dt.uint32), T[tc][:, 0:NP].bitcast(dt.uint32).indirect(T[ls][:, l:l + n // 8])), tab)
                 add("pz" + s, "F", ("g", 2 * n), ndep, lambda e, T, k, on, o=o, n=n, l=l, ts=ts, pz=pz, ls=ls:
                     move(e, on, T[pz][:, 2 * o:2 * (o + n)], T[ts][:, 0:NP].indirect(T[ls][:, l:l + n // 8])), tab)
-                pn = ["pc" + s, "pz" + s]
             for b in range(4):
                 bk = "%d_%s" % (b, s)
 
-                def state(e, T, k, on, b=b, t=t, o=o, n=n):
+                def state(e, T, k, on, b=b, h=h, n=n):
                     return e.matmul_mx(T.ps[:, 512 * k:512 * k + n], T.ec[:, 128 * b:128 * b + 128], T.es[:, 128 * b:128 * b + 128],
-                                       T["sc%d" % t][:, o:o + n], T["ss%d" % t][:, o:o + n], on, not on)
+                                       T.sc[:, h:h + n], T.ss[:, h:h + n], on, not on)
 
                 def nodes(e, T, k, on, b=b, t=t, o=o, n=n, pc=pc, pz=pz):
                     out = T.ps[:, 512 * k:512 * k + n]
@@ -142,109 +141,95 @@ def make_ops(cnt):
                 add("n" + bk, "P", ("p2" if t else "p1", n), pn + ["f%d" % b if t else "e%d" % b], nodes, bank="b" + bk)
                 add("cv" + bk, "F", ("c", n), ["a" + bk, "n" + bk], lambda e, T, k, on, b=b, t=t, o=o, n=n:
                     move(e, on, T["bt%d" % t][:, 4 * o + b:4 * (o + n):4], T.ps[:, 512 * k:512 * k + n], 0.5), bank="b" + bk)
-            add("qv" + s, "V", ("q", n), ["cv%d_%s" % (b, s) for b in range(4)], lambda e, T, k, on, t=t, o=o, n=n:
-                e.quantize_mx(T["vc%d" % t][:, o:o + n], T["vs%d" % t][:, o:o + n], T["bt%d" % t][:, 4 * o:4 * (o + n)]))
-            add("sc" + s, "P", ("p1", n), ["qv" + s] + (["qu"] if t == 0 else []), lambda e, T, k, on, t=t, o=o, n=n, tc=tc, ts=ts:
-                e.matmul_mx(T.ps[:, 512 * k:512 * k + n], T[tc][:, NP:TW], T[ts][:, NP:TW], T["vc%d" % t][:, o:o + n], T["vs%d" % t][:, o:o + n], True, True), utab, "s" + s)
+            add("qv" + s, "V", ("q", n), ["cv%d_%s" % (b, s) for b in range(4)], lambda e, T, k, on, t=t, o=o, n=n, h=h:
+                e.quantize_mx(T.vc[:, h:h + n], T.vs[:, h:h + n], T["bt%d" % t][:, 4 * o:4 * (o + n)]))
             for b in range(4):
                 bk = "%d_%s" % (b, s)
-                add("l" + bk, "P", ("p1", n), ["qv" + s], lambda e, T, k, on, b=b, t=t, o=o, n=n:
-                    e.matmul_mx(T.ps[:, 512 * k:512 * k + n], T.wqc[:, 128 * b:128 * b + 128], T.wqs[:, 128 * b:128 * b + 128], T["vc%d" % t][:, o:o + n], T["vs%d" % t][:, o:o + n], True, True),
+                add("l" + bk, "P", ("p1", n), ["qv" + s], lambda e, T, k, on, b=b, h=h, n=n:
+                    e.matmul_mx(T.ps[:, 512 * k:512 * k + n], T.wqc[:, 128 * b:128 * b + 128], T.wqs[:, 128 * b:128 * b + 128], T.vc[:, h:h + n], T.vs[:, h:h + n], True, True),
                     [("lw", 32)], "l" + bk)
-                add("cr" + bk, "F", ("c", n), ["l" + bk], lambda e, T, k, on, b=b, t=t, o=o, n=n:
-                    move(e, on, T["lt%d" % t][:, 4 * o + b:4 * (o + n):4], T.ps[:, 512 * k:512 * k + n], 0.03125), bank="l" + bk)
-            add("qs%d_%d" % (t + 1, c), "V", ("q", n), ["cr%d_%s" % (b, s) for b in range(4)], lambda e, T, k, on, t=t, o=o, n=n:
-                e.quantize_mx(T["sc%d" % (t + 1)][:, o:o + n], T["ss%d" % (t + 1)][:, o:o + n], T["lt%d" % t][:, 4 * o:4 * (o + n)]))
+                add("cr" + bk, "F", ("c", n), ["l" + bk], lambda e, T, k, on, b=b, h=h, n=n:
+                    move(e, on, T.lt[:, 4 * h + b:4 * (h + n):4], T.ps[:, 512 * k:512 * k + n], 0.03125), bank="l" + bk)
+            add("qs%d_%d" % (t + 1, c), "V", ("q", n), ["cr%d_%s" % (b, s) for b in range(4)], lambda e, T, k, on, h=h, n=n:
+                e.quantize_mx(T.sc[:, NT + h:NT + h + n], T.ss[:, NT + h:NT + h + n], T.lt[:, 4 * h:4 * (h + n)]))
+            add("sc" + s, "P", ("p1", n), ["qv" + s] + (["qu"] if t == 0 else []), lambda e, T, k, on, h=h, n=n, tc=tc, ts=ts:
+                e.matmul_mx(T.ps[:, 512 * k:512 * k + n], T[tc][:, NP:TW], T[ts][:, NP:TW], T.vc[:, h:h + n], T.vs[:, h:h + n], True, True), utab, "s" + s)
             add("sg" + s, "S", ("c", n), ["sc" + s, "bi"], lambda e, T, k, on, t=t, o=o, n=n:
                 e.activation(T["sg%d" % t][:, o:o + n], T.ps[:, 512 * k:512 * k + n], F.Sign, bias=T.bias[:, 0:1], scale=T.rt[:, 0:1]), bank="s" + s)
-            m = o + 16 * (c + 1)
-            add("mg" + s, "V", ("g", n), ["sg" + s, "mi"] + ndep, lambda e, T, k, on, t=t, o=o, n=n, m=m, ls=ls, nat=nat, nq=nq:
-                e.tensor_tensor(T.mm[:, m:m + n], T["win%d" % (t % 2)][:].indirect(T[ls][:, nat:nat + nq]), T["sg%d" % t][:, o:o + n], A.mult), [("w%d" % t, 32)])
-            if t < NH - 1:
-                z, to, lc = 40 * (NC * t + c), 2 * o + 32 * c, 4 * KINDS.index(n)
-                add("t1" + s, "V", ("h", n), ["mg" + s], lambda e, T, k, on, n=n, m=m, to=to: e.transpose(T.tt[:, to:to + n], T.mm[:, m:m + n]))
-                add("t2" + s, "V", ("h", n + 32), ["mg" + s], lambda e, T, k, on, n=n, m=m, to=to: e.transpose(T.tt[:, to + n:to + 2 * n + 32], T.mm[:, m - 16:m + n + 16]))
-                add("mx" + s, "V", ("c", 8 * nb + 4), ["t1" + s, "t2" + s], lambda e, T, k, on, n=n, to=to, z=z, nb=nb:
-                    e.tensor_tensor(T.zc[:, z:z + 4 * nb + 2], T.tt[:, to:to + 2 * n + 32:16], T.tt[:, to + 1:to + 2 * n + 32:16], A.add))
-                add("cp" + s, "V", ("g", 48), ["mx" + s, "cl%d" % n], lambda e, T, k, on, t=t, c=c, z=z, nb=nb, lc=lc:
-                    e.tensor_copy(T["lst%d" % (t + 1)][:, 48 * c:48 * c + 48], T.zc[:, z:z + 4 * nb + 2].indirect(T.cl[:, lc:lc + 3])))
-            else:
-                add("t1" + s, "V", ("h", n), ["mg" + s], lambda e, T, k, on, o=o, n=n, m=m: e.transpose(T.tl[:, o:o + n], T.mm[:, m:m + n]))
-                add("y%d" % c, "P", ("p1", n), ["qs3_%d" % c, "qv"], lambda e, T, k, on, o=o, n=n:
-                    e.matmul_mx(T.ps[:, 512 * k:512 * k + n], T.qvc[:], T.qvs[:], T.sc3[:, o:o + n], T.ss3[:, o:o + n], True, True), bank="y%d" % c)
-                add("cy%d" % c, "F", ("c", n), ["y%d" % c], lambda e, T, k, on, o=o, n=n: move(e, on, T.ysb[:, o:o + n], T.ps[:, 512 * k:512 * k + n]), bank="y%d" % c)
-    tl = ["t1%d_%d" % (NH - 1, c) for c in range(NC)]
+            mm, m = ("mm", o + 16 * (c + 1)) if t < NH - 1 else ("ml", o)
+            add("mg" + s, "V", ("g", n), ["sg" + s, "mi"] + ndep, lambda e, T, k, on, t=t, o=o, n=n, mm=mm, m=m, ls=ls, nat=nat, nq=nq:
+                e.tensor_tensor(T[mm][:, m:m + n], T["win%d" % (t % 2)][:].indirect(T[ls][:, nat:nat + nq]), T["sg%d" % t][:, o:o + n], A.mult), [("w%d" % t, 32)])
+            if t == NH - 1:
+                add("t1" + s, "V", ("h", n), ["mg" + s], lambda e, T, k, on, o=o, n=n: e.transpose(T.tl[:, o:o + n], T.ml[:, o:o + n]))
+                continue
+            z, to, lc = 40 * (NC * t + c), 2 * o + 32 * c, 2 * KINDS.index(n)
+            add("t1" + s, "V", ("h", n), ["mg" + s], lambda e, T, k, on, n=n, m=m, to=to: e.transpose(T.tt[:, to:to + n], T.mm[:, m:m + n]))
+            add("t2" + s, "V", ("h", n + 32), ["mg" + s], lambda e, T, k, on, n=n, m=m, to=to: e.transpose(T.tt[:, to + n:to + 2 * n + 32], T.mm[:, m - 16:m + n + 16]))
+            add("mx" + s, "V", ("c", 8 * nb + 4), ["t1" + s, "t2" + s], lambda e, T, k, on, n=n, to=to, z=z, nb=nb:
+                e.tensor_tensor(T.zc[:, z:z + 4 * nb + 2], T.tt[:, to:to + 2 * n + 32:16], T.tt[:, to + 1:to + 2 * n + 32:16], A.add))
+            add("cp" + s, "V", ("g", 32), ["mx" + s, "cl%d" % n], lambda e, T, k, on, t=t, c=c, z=z, nb=nb, lc=lc:
+                e.tensor_copy(T["lst%d" % (t + 1)][:, 32 * c:32 * c + 32], T.zc[:, z:z + 4 * nb + 2].indirect(T.cl[:, lc:lc + 2])))
+    for i, cs in enumerate(YSEG):
+        o, n = span(cs)
+        add("y%d" % i, "P", ("p1", n), ["qs3_%d" % c for c in cs] + ["qv"], lambda e, T, k, on, h=NH * NT + o, n=n:
+            e.matmul_mx(T.ps[:, 512 * k:512 * k + n], T.qvc[:], T.qvs[:], T.sc[:, h:h + n], T.ss[:, h:h + n], True, True), bank="y%d" % i)
+        add("cy%d" % i, "F", ("c", n), ["y%d" % i], lambda e, T, k, on, o=o, n=n: move(e, on, T.ysb[:, o:o + n], T.ps[:, 512 * k:512 * k + n]), bank="y%d" % i)
+    tl = ["t1%d_%d" % (NH - 1, c) for c in range(NC)] + ["nx0", "nx1"]
     for h in range(2):
-        add("fm%d" % h, "V", ("c", 28), tl, lambda e, T, k, on, h=h: e.tensor_tensor(T.zf[:, 14 * h:14 * h + 14], T.tl[:, 16 * h:NT:32], T.tl[:, 16 * h + 1:NT:32], A.add))
-    add("ft", "V", ("c", 32), ["fm0", "fm1", "zi"], lambda e, T, k, on: e.transpose(T.zo[:], T.zf[:]))
+        add("fm%d" % h, "V", ("c", 28), tl, lambda e, T, k, on, h=h: e.tensor_tensor(T.nxh[:, 14 * h:14 * h + 14], T.tl[:, 16 * h:NT:32], T.tl[:, 16 * h + 1:NT:32], A.add))
+    add("ft", "V", ("c", 32), ["fm0", "fm1"], lambda e, T, k, on: e.transpose(T.zo[:], T.nxh[:, 0:32]))
     return ops
-
-
-def bits(engines):
-    return sum(1 << e for e in engines)
 
 
 def plan(T, topo):
     cores, n = list(T.cores), len(T.cores)
     calls, got = {}, {}
 
-    def put(src, item):
-        calls.setdefault(src, []).append(item)
-
-    def send(src, dst, a, b, c0, c1, sem, eng):
-        for kind in "cs":
-            s = sem if isinstance(sem, str) else sem[kind]
-            put(src, ("send", dst, kind, a, b, c0, c1, s, eng))
+    def call(src, need, *transfers):
+        calls.setdefault(src, []).append((need, transfers))
+        for dst, a, b, c0, c1, s, eng in transfers:
             got[(dst, s)] = got.get((dst, s), 0) + len(eng)
             got[(src, "sent")] = got.get((src, "sent"), 0) + len(eng)
 
     for r in range(n):
-        me, d1, d2 = cores[r], cores[(r - 1) % n], cores[(r - 2) % n]
-        near = topo.chip(d1) == topo.chip(me)
+        me, d1, d2, up = cores[r], cores[(r - 1) % n], cores[(r - 2) % n], cores[(r + 1) % n]
         off = topo.engines(me, d2)
-        other = [c for c in topo.cores_of(me) if c != me][0]
-        rest = [e for e in topo.engines(me, other) if e not in off]
-        e1, e2 = (rest, off) if near else (off[:len(off) // 2], off[len(off) // 2:])
-        put(me, ("nx", d1, d2, e1, e2))
-        got[(d1, "n1")], got[(d2, "n2")] = len(e1), len(e2)
-        got[(me, "sent")] = got.get((me, "sent"), 0) + len(e1) + len(e2)
-        put(me, ("wait", ["qa"]))
-        if near:
-            first = topo.engines(me, d1)
-            send(me, d1, "t0", "t1", 0, HALF, "k1", first)
+        every = topo.engines(me, [c for c in topo.cores_of(me) if c != me][0])
+        rest = [e for e in every if e not in off]
+        kids, q = ["nx0", "nx1"], len(off) // 2
+        if topo.chip(d1) == topo.chip(me):
+            call(me, kids, (d1, "nxa0", "nxa1", 0, 80, "n1", rest), (d2, "nxa0", "nxa2", 0, 80, "n2", off))
+            call(me, ["qa", "qb", "qu"], (d1, "tc0", "tc1", 0, TW, "ka1", every))
+            call(me, [], (d1, "ts0", "ts1", 0, TW, "kb1", every))
+            call(me, ["hr"], (d2, "tch", "tc1", REL, HALF, "kr1", off))
+            call(me, [], (d2, "tc0", "tc2", 0, HALF, "k2", off))
+            call(me, ["fill", "ka1", "kr1", "kb1"], (d1, "tc1", "tc2", 0, NP, "k2", rest))
+            call(me, [], (d1, "ts1", "ts2", 0, TW, "k2", rest), (d2, "ts0", "ts2", 0, TW, "k2", off))
+            call(me, ["u1"], (d1, "tc1", "tc2", NP, TW, "u2", rest))
         else:
-            first = off
-            h = [c for c in topo.cores_of(me) if c not in cores and topo.die(c) != topo.die(me) and topo.may_write(c, d1)][0]
-            send(me, h, "t0", "h", 0, HALF, {"c": "hcod", "s": "hsca"}, rest)
-            send(h, d1, "h", "t1", 0, HALF, "k1", topo.engines(h, d1))
-            calls[h] = [("sem", "hcod"), calls[h][0], ("sem", "hsca"), calls[h][1]]
-        put(me, ("iota", 0))
-        put(me, ("wait", ["qb"]))
-        send(me, d1, "t0", "t1", HALF, NP, "k1", first)
-        put(me, ("wait", ["qu"]))
-        send(me, d1, "t0", "t1", NP, TW, "u1", first)
-        put(me, ("sem", "k1"))
-        if near:
-            send(me, d2, "t0", "t2", 0, CUT, "k2", off)
-            put(me, ("sem", "u1"))
-            send(me, d1, "t1", "t2", 0, TW, "k2", rest)
-        else:
-            put(me, ("sem", "u1"))
-            send(me, d1, "t1", "t2", CUT, TW, "k2", off)
+            call(me, kids, (d1, "nxa0", "nxa1", 0, 80, "n1", off))
+            call(me, ["qa"], (d1, "tc0", "tc1", 0, REL, "ka1", off), (up, "tc0", "tch", REL, HALF, "hr", rest))
+            call(me, ["qb", "qu"], (d1, "tc0", "tc1", HALF, NP, "kb1", off[:q]), (d1, "ts0", "ts1", 0, TW, "kb1", off[q:]))
+            call(me, [], (d1, "tc0", "tc1", NP, TW, "u1", off))
+            call(me, [], (d2, "nxa0", "nxa2", 0, 80, "n2", off))
+            call(me, ["fill", "ka1"], (d1, "tc1", "tc2", HALF, TW, "k2", off))
     return calls, got
-
-
-BUF = {"t0": ("tc0", "ts0"), "t1": ("tc1", "ts1"), "t2": ("tc2", "ts2"), "h": ("hc", "hs")}
 
 
 def list_rows():
     rows = []
     for i, n in enumerate(KINDS):
-        nb = n // 32
-        for l, (q, hs) in enumerate(((n // 16 - 16, (0, 0)), (0, (1, 1)), (0, (0, 1)))):
-            a = 64 + 96 * i + 32 * l
-            rows.append((a, [[2, 8], [2 * nb + 2, 2]], q + hs[0]))
-            rows.append((a + 16, [[2, 8], [-2 * nb, 2]], 2 * nb + q + hs[1]))
+        nb, nq = n // 32, n // 16
+        for h in range(2):
+            step, base, e = (-2 * nb, 2 * nb, 0) if h else (2 * nb + 2, 0, 0)
+            if 2 * nq == 16:
+                rows.append((64 + 64 * i + 16 * h, [[1, 2], [2, nq // 2], [step, 2]], base))
+                e = 16
+            while e < 32:
+                l = min(e // nq, 2)
+                end = min(e // 16 * 16 + 16, (l + 1) * nq if l < 2 else 32)
+                rows.append((64 + 64 * i + 32 * (e // 16) + 16 * h + e % 16, [[2, (end - e) // 2], [step, 2]], base + e - l * nq + (0, 1, h)[l]))
+                e = end
     return rows
 
 
@@ -297,111 +282,99 @@ def waits(order, idx, by, before):
 
 
 def rank_program(g, core, T, topo):
+    if T.rank_of(core) is None:
+        return
     calls, got = plan(T, topo)
-    rank = T.rank_of(core)
-    sem, CH = T.sem, chunks()
-    idx = {}
-    rows = list_rows()
+    sem = T.sem
+    ops = make_ops({s: got.get((core, s), 0) for s in SEMAPHORES})
+    by = {o["name"]: o for o in ops}
+    order, bank, before, opens = lay_out(ops, ORDER.split())
+    idx = {n: (e, i + 1) for e in order for i, n in enumerate(order[e])}
+    todo = waits(order, idx, by, before)
 
-    def iota(a, pat, base):
-        g.iota(T.rr[:, a:a + pat[0][1] * pat[1][1]], pat, base, 0, allow_small_or_imprecise_dtypes=True).then_inc(sem.G, 1)
+    def waiter(q):
+        seen = {}
 
-    if rank is not None:
-        ops = make_ops({s: got[(core, s)] for s in ("k1", "u1", "k2")})
-        by = {o["name"]: o for o in ops}
-        order, bank, before, opens = lay_out(ops, ORDER.split())
+        def need(s, v):
+            if seen.get(s, 0) < v:
+                q.wait_ge(sem[s], v)
+                seen[s] = v
+        return need
+
+    def after(need, ds):
         for e in order:
-            for i, n in enumerate(order[e]):
-                idx[n] = (e, i + 1)
-        todo = waits(order, idx, by, before)
+            need(e, max([0] + [idx[d][1] for d in ds if idx[d][0] == e]))
 
-        def waiter(q):
-            seen = {}
+    sy, sc = g.sync, g.scalar
+    sc.dma_start(T.nxl[:], T.nx[:]).then_inc(sem.lnx, 16)
+    sc.dma_start(T.stw[:], T.st[:]).then_inc(sem.lst, 16)
+    ns = waiter(sy)
+    loads = {"ka": [(T.kt[:, 0:4 * HALF], T.k[:, 0:4 * HALF], "ka")], "kb": [(T.kt[:, 4 * HALF:4 * NP], T.k[:, 4 * HALF:4 * NP], "kb")],
+             "u": [(T.ut[:], T.u[:], "lu")], "v": [(T.vtile[:], T.v[:], "lv")],
+             "W": [(T.wqc[:].bitcast(dt.uint8), T.wc[:], "lw"), (T.wqs[:], T.ws[:], "lw")]}
+    for c in range(NC):
+        o, n = span([c])
+        loads["x%d" % c] = [(T.xt[:, 4 * o:4 * (o + n)], T.x[:, 4 * o:4 * (o + n)], "x%d" % c)]
+    for t in range(NH):
+        loads["w%d" % t] = [(T["win%d" % (t % 2)][b:128:16, :], T["nxa%d" % t][:, 40 * b:40 * b + 40], "w%d" % t) for b in range(2)]
+    for x in LOADS.split():
+        if x in ("w0", "w1", "w2"):
+            after(ns, {"w0": ["wi0", "nx0", "nx1"], "w1": [], "w2": ["mg0_%d" % c for c in range(NC)]}[x])
+            if x != "w0":
+                ns("G", 4 + len(list_rows()))
+                ns("n" + x[1], got[(core, "n" + x[1])])
+        for dst, src, s in loads[x]:
+            sy.dma_start(dst, src).then_inc(sem[s], 16)
 
-            def need(s, v):
-                if seen.get(s, 0) < v:
-                    q.wait_ge(sem[s], v)
-                    seen[s] = v
-            return need
+    stores, last = {}, NH * NT
+    for i, cs in enumerate(YSEG):
+        o, n = span(cs)
+        stores["oc%d" % i] = (["qs3_%d" % c for c in cs], T.oc[:, 4 * o:4 * (o + n)], T.sc[:, last + o:last + o + n].bitcast(dt.uint8))
+        stores["y%d" % i] = (["cy%d" % i], T.y[:, o:o + n], T.ysb[:, o:o + n])
+    for a in range(4):
+        stores["os%d" % a] = (["qs3_%d" % c for c in range(NC)], T.osc[4 * a:4 * a + 4, :], T.ss[32 * a:32 * a + 4, last:last + NT])
+        stores["pl%d" % a] = (["ft"], T.pl[2 * a:2 * a + 2, :], T.zo[32 * a:32 * a + 28, :])
 
-        def after(need, ds):
-            for e in order:
-                need(e, max([0] + [idx[d][1] for d in ds if idx[d][0] == e]))
+    def store(q, need, names):
+        for x in names.split():
+            ds, dst, src = stores[x]
+            after(need, ds)
+            q.dma_start(dst, src).then_inc(sem.out, 16)
 
-        sy, sc = g.sync, g.scalar
-        sc.dma_start(T.nxl[:], T.nx[:]).then_inc(sem.lnx, 16)
-        sc.dma_start(T.stw[:], T.st[:]).then_inc(sem.lst, 16)
-        ns = waiter(sy)
-        loads = {"ka": [(T.kt[:, 0:4 * HALF], T.k[:, 0:4 * HALF], "ka")], "kb": [(T.kt[:, 4 * HALF:4 * NP], T.k[:, 4 * HALF:4 * NP], "kb")],
-                 "u": [(T.ut[:], T.u[:], "lu")], "v": [(T.vtile[:], T.v[:], "lv")],
-                 "W": [(T.wqc[:].bitcast(dt.uint8), T.wc[:], "lw"), (T.wqs[:], T.ws[:], "lw")]}
-        for c, (o, n) in enumerate(CH):
-            loads["x%d" % c] = [(T.xt[:, 4 * o:4 * (o + n)], T.x[:, 4 * o:4 * (o + n)], "x%d" % c)]
-        for t in range(NH):
-            loads["w%d" % t] = [(T["win%d" % (t % 2)][b:128:16, :], T["nxa%d" % t][:, 40 * b:40 * b + 40], "w%d" % t) for b in range(2)]
-        for x in LOADS.split():
-            if x in ("w0", "w1", "w2"):
-                after(ns, {"w0": ["wi0", "nx0", "nx1"], "w1": ["wi1"], "w2": ["mg0_%d" % c for c in range(NC)]}[x])
-                if x != "w0":
-                    ns("n" + x[1], got[(core, "n" + x[1])])
-            for dst, src, s in loads[x]:
-                sy.dma_start(dst, src).then_inc(sem[s], 16)
+    for e, q in (("P", g.tensor), ("V", g.vector), ("S", g.scalar)):
+        for n in order[e]:
+            for s, v in todo[n].items():
+                q.wait_ge(sem[s], v)
+            by[n]["fn"](q, T, bank.get(by[n]["bank"]), opens[n] if e == "P" else e).then_inc(sem[e], 1)
+        if e == "S":
+            store(q, waiter(q), STORES[1])
+    store(sy, ns, STORES[0])
+    for e in order:
+        ns(e, len(order[e]))
+    ns("out", 16 * len(stores))
 
-        stores = {}
-        for c, (o, n) in enumerate(CH):
-            stores["oc%d" % c] = (["qs3_%d" % c], T.oc[:, 4 * o:4 * (o + n)], T.sc3[:, o:o + n].bitcast(dt.uint8))
-            stores["y%d" % c] = (["cy%d" % c], T.y[:, o:o + n], T.ysb[:, o:o + n])
-        for a in range(4):
-            stores["os%d" % a] = (["qs3_%d" % c for c in range(NC)], T.osc[4 * a:4 * a + 4, :], T.ss3[32 * a:32 * a + 4, :])
-            stores["pl%d" % a] = (["ft"], T.pl[2 * a:2 * a + 2, :], T.zo[32 * a:32 * a + 28, :])
+    def iota(out, pat, base, mult=0):
+        g.iota(out, pat, base, mult, allow_small_or_imprecise_dtypes=True).then_inc(sem.G, 1)
 
-        def store(q, need, names):
-            for x in names.split():
-                ds, dst, src = stores[x]
-                after(need, ds)
-                q.dma_start(dst, src).then_inc(sem.out, 16)
+    iota(T.ib[:], [[-1, 128]], 0, 1)
+    iota(T.rr[:, 0:32], [[0, 2], [-1, 16]], 1)
+    iota(T.rr[:, 32:64], [[-1, 2], [0, 16]], 0)
+    for a, pat, base in list_rows():
+        iota(T.rr[:, a:a + math.prod(c for s, c in pat)], pat, base)
 
-        for e, q in (("P", g.tensor), ("V", g.vector), ("S", g.scalar)):
-            for n in order[e]:
-                for s, v in todo[n].items():
-                    q.wait_ge(sem[s], v)
-                by[n]["fn"](q, T, bank.get(by[n]["bank"]), opens[n] if e == "P" else e).then_inc(sem[e], 1)
-            if e == "S":
-                store(q, waiter(q), STORES[1])
-        store(sy, ns, STORES[0])
-        for e in order:
-            ns(e, len(order[e]))
-        ns("out", 16 * len(stores))
-
-        g.iota(T.ib[:], [[-1, 128]], 0, 1, allow_small_or_imprecise_dtypes=True).then_inc(sem.G, 1)
-        iota(0, [[0, 2], [-1, 16]], 1)
-        iota(32, [[-1, 2], [0, 16]], 0)
-        for p in rows[:EARLY]:
-            iota(*p)
-
-    for it in calls.get(core, []):
-        if it[0] == "nx":
-            g.wait_ge(sem.V, max(idx["nx0"][1], idx["nx1"][1]))
-            tr = []
-            for d, eng, name in ((it[1], it[3], "1"), (it[2], it[4], "2")):
-                rid, pid, se = topo.addr(d)
-                tr.append(RemoteDMATransfer(dst_ids=[DstId(rid=rid, pnc=pid)], dma_engine_mask=bits(eng), remote_sem=sem["n" + name], src=T.nxa0[:], dst=T["nxa" + name][:]))
-            g.remote_dma_fused(tr, local_sem=sem.sent)
-        elif it[0] == "wait":
-            for d in it[1]:
-                g.wait_ge(sem[idx[d][0]], idx[d][1])
-        elif it[0] == "sem":
-            g.wait_ge(sem[it[1]], got[(core, it[1])])
-        elif it[0] == "iota":
-            for p in rows[EARLY:]:
-                iota(*p)
-        else:
-            x, d, kind, a, b, c0, c1, s, eng = it
+    ng = waiter(g)
+    for need, transfers in calls[core]:
+        for d in need:
+            if d == "fill":
+                iota(T.win1[:], [[0, NP]], 0)
+            else:
+                ng(*idx.get(d, (d, got.get((core, d), 0))))
+        tr = []
+        for d, a, b, c0, c1, s, eng in transfers:
             rid, pid, se = topo.addr(d)
-            i = 0 if kind == "c" else 1
-            src, dst = T[BUF[a][i]][:, c0:c1], T[BUF[b][i]][:, c0:c1]
-            if kind == "c":
+            src, dst = T[a][:, c0:c1], T[b][:, c0:c1]
+            if a[:2] == "tc":
                 src, dst = src.bitcast(dt.uint8), dst.bitcast(dt.uint8)
-            g.remote_dma(dst, src, sem[s], sem.sent, pid, rid, bits(eng))
-    if (core, "sent") in got:
-        g.wait_ge(sem.sent, got[(core, "sent")])
+            tr.append(RemoteDMATransfer(dst_ids=[DstId(rid=rid, pnc=pid)], dma_engine_mask=sum(1 << e for e in eng), remote_sem=sem[s], src=src, dst=dst))
+        g.remote_dma_fused(tr, local_sem=sem.sent)
+    ng("sent", got[(core, "sent")])

import math
from concourse.bass import DstId, RemoteDMATransfer
from concourse.mybir import dt, AluOpType, ActivationFunctionType

NT, NP, NH = 448, 640, 3
SIZES = [160, 160, 128]
HALF = 448
TW = NP + 128
TINY = 2.0 ** -120
X4, U8 = "float8_e4m3fn_x4", "uint8"
ORDER = "mz df e1 wi0 ra mi nh de do e3 e2 nx0 nx1 s3 s1 s0 qa s2 qb g1_0 g0_0 g2_0 qu g3_0* g0_1 g2_1 g3_1 qs0_0 e0 qn0 a3_0_0 a0_0_0 a1_0_0 n3_0_0 qs0_1 sn bi g1_1* f0 n2_0_0 a2_0_0 a2_0_1 n1_0_0 n0_0_0 cv3_0_0 cv2_0_0 qn1 f3 qn2 cv1_0_0 cv0_0_0 a0_0_1 a3_0_1 a1_0_1 qs0_2 n3_0_1 n1_0_1 qv0_0 cv3_0_1 cv1_0_1 rb f2 n0_0_1 n2_0_1 n2_0_2 cv0_0_1 cv2_0_1 n3_0_2 sc0_0 a2_0_2 cl160 f1 cl128 sg0_0 qv0_1 a3_0_2 n0_0_2 a1_0_2 n1_0_2 a0_0_2 l2_0_0 cv2_0_2 cv3_0_2 cv1_0_2 mg0_0 l0_0_0 cr2_0_0* sc0_1 cv0_0_2 l3_0_0 cr0_0_0 t20_0 t10_0 l1_0_0 l3_0_1 qv0_2 sg0_1 l1_0_1 cr1_0_0* cr3_0_0 l2_0_1 l0_0_1 mx0_0 cr3_0_1 mg0_1 l1_0_2 sc0_2 l3_0_2 l2_0_2 cr1_0_1 cp0_0 cr2_0_1 cr0_0_1 qs1_0 t10_1 t20_1 sg0_2 pc1_0 pz1_0 a2_1_0 a3_1_0 l0_0_2 cr0_0_2 cr3_0_2 a1_1_0 a0_1_0 mx0_1 mg0_2 n3_1_0 n1_1_0 n2_1_0 cp0_1 cr2_0_2 cr1_0_2 qs1_1 t10_2 t20_2 pc1_1 pz1_1 mx0_2 n0_1_0 a1_1_1 a0_1_1 a2_1_1 a3_1_1 cv2_1_0* cv1_1_0* cv3_1_0 cv0_1_0 cp0_2 qs1_2 qv1_0 pc1_2 n3_1_1 cv3_1_1 pz1_2 n1_1_1 cv1_1_1* n2_1_1 n0_1_1 cv0_1_1* sc1_0 cv2_1_1 a1_1_2 l0_1_0 cr0_1_0* l2_1_0 l1_1_0 sg1_0 n1_1_2 qv1_1 cr2_1_0 a2_1_2 l3_1_0 n2_1_2 mg1_0 cr1_1_0 cr3_1_0 cv1_1_2 n0_1_2 cv2_1_2* sc1_1 sg1_1 t21_0 t11_0 l3_1_1 a0_1_2 qs2_0 n3_1_2 cr3_1_1 cv0_1_2* a3_1_2 mx1_0 l2_1_1 mg1_1 l1_1_1 cv3_1_2 l0_1_1 a3_2_0 a0_2_0 a1_2_0 cr2_1_1 cp1_0 qv1_2 cr1_1_1 t21_1 t11_1 cr0_1_1 pc2_0 pz2_0 a2_2_0 l2_1_2 sc1_2 sg1_2 l3_1_2 l1_1_2 mx1_1 qs2_1 cp1_1 mg1_2 n0_2_0 cr3_1_2 cr2_1_2 cr1_1_2 pc2_1 pz2_1 t11_2 t21_2 cv0_2_0* l0_1_2 n2_2_0 n3_2_0 a2_2_1 n1_2_0 a1_2_1 mx1_2 cr0_1_2 cv3_2_0 n2_2_1 cv2_2_0 cv1_2_0* n1_2_1 cp1_2 cv2_2_1 qs2_2 a0_2_1 n0_2_1 n3_2_1 a3_2_1 qv2_0 cv1_2_1 pc2_2 pz2_2 cv3_2_1* a3_2_2 a1_2_2 qv cv0_2_1 qv2_1 sc2_0 sg2_0 mg2_0 l0_2_0 a2_2_2 a0_2_2 cr0_2_0 n2_2_2 n0_2_2 cv2_2_2 cv0_2_2 n3_2_2 cv3_2_2* n1_2_2 l3_2_1 cr3_2_1 l3_2_0 cv1_2_2* l1_2_0 cr3_2_0* l2_2_1 l2_2_0 cr1_2_0 qv2_2 l0_2_1 cr2_2_1 l1_2_1 cr2_2_0* sc2_1 cr0_2_1 sc2_2 cr1_2_1* sg2_1 qs3_0 l3_2_2 l2_2_2 sg2_2 qs3_1 l1_2_2 l0_2_2 cr2_2_2 cr3_2_2* mg2_1 mg2_2 cr1_2_2 cr0_2_2 qs3_2 y0 cy0 y1 t12_0 t12_1 t12_2 fm1 fm0 ft cy1"
LOADS = "ka kb u x0 x1 W x2 w0 w1 v w2"
GSEG = [[0], [1, 2]]
YSEG = [[0, 1], [2]]
STORES = ["oc0 y0 oc1 os1 os3 y1 pl1 pl3", "os0 os2 pl0 pl2"]
REL = HALF // 2
KINDS = sorted(set(SIZES), reverse=True)
NC = len(SIZES)

SCRATCH = {
    "ps": ("psum", [128, 4096], "float32"),
    "kt": ("sbuf", [128, 4 * NP], "bfloat16"), "xt": ("sbuf", [128, 4 * NT], "bfloat16"), "nt": ("sbuf", [128, 4 * NT], "bfloat16"),
    "ut": ("sbuf", [128, 512], "bfloat16"), "vtile": ("sbuf", [128, 512], "bfloat16"),
    "qvc": ("sbuf", [128, 128], X4), "qvs": ("sbuf", [128, 128], U8),
    "wqc": ("sbuf", [128, 512], X4), "wqs": ("sbuf", [128, 512], U8),
    "zt": ("sbuf", [128, 1672], "bfloat16"), "ib": ("sbuf", [128, 128], "float32"),
    "ec": ("sbuf", [128, 1536], X4), "es": ("sbuf", [128, 1536], U8),
    "rr": ("sbuf", [128, 64 + 64 * len(KINDS)], "float32"), "rt": ("sbuf", [128, 64 + 64 * len(KINDS)], "float32"),
    "cl": ("sbuf", [128, 2 * len(KINDS)], "uint16"), "bias": ("sbuf", [128, 1], "float32"),
    "stw": ("sbuf", [128, 28], "int32"), "lst0": ("sbuf", [128, 140], "uint16"),
    "lst1": ("sbuf", [128, 32 * NC], "uint16"), "lst2": ("sbuf", [128, 32 * NC], "uint16"),
    "nxl": ("sbuf", [128, 80], "int32"), "nxh": ("sbuf", [128, 80], "float32"), "nxa0": ("sbuf", [128, 80], "float32"),
    "nxa1": ("sbuf", [128, 80], "float32"), "nxa2": ("sbuf", [128, 80], "float32"),
    "win0": ("sbuf", [128, NP], "float32"), "win1": ("sbuf", [128, NP], "float32"),
    "mm": ("sbuf", [128, NT + 16 * NC + 16], "float16"), "tt": ("sbuf", [128, 2 * NT + 32 * NC], "float16"), "tl": ("sbuf", [128, NT], "float16"),
    "zc": ("sbuf", [128, 80 * NC], "float32"), "zo": ("sbuf", [128, 32], "float32"),
    "ysb": ("sbuf", [128, NT], "float32"), "tch": ("sbuf", [128, HALF], X4),
    "sc": ("sbuf", [128, (NH + 1) * NT], X4), "ss": ("sbuf", [128, (NH + 1) * NT], U8),
    "vc": ("sbuf", [128, NH * NT], X4), "vs": ("sbuf", [128, NH * NT], U8),
    "lt": ("sbuf", [128, 4 * NH * NT], "bfloat16"), "ml": ("sbuf", [128, NT], "float16"),
}
for _t in range(NH):
    SCRATCH["tc%d" % _t] = ("sbuf", [128, TW], X4)
    SCRATCH["ts%d" % _t] = ("sbuf", [128, TW], U8)
    SCRATCH["pc%d" % _t] = ("sbuf", [128, 2 * NT], X4)
    SCRATCH["pz%d" % _t] = ("sbuf", [128, 2 * NT], U8)
    SCRATCH["bt%d" % _t] = ("sbuf", [128, 4 * NT], "bfloat16")
    SCRATCH["sg%d" % _t] = ("sbuf", [128, NT], "bfloat16")

SEMAPHORES = ["P", "V", "S", "G", "ka", "kb", "x0", "x1", "x2", "lu", "lw", "lv", "lst", "lnx", "w0", "w1", "w2",
              "hr", "ka1", "kr1", "kb1", "u1", "k2", "u2", "n1", "n2", "sent", "out"]


def span(cs):
    return sum(SIZES[:cs[0]]), sum(SIZES[c] for c in cs)


def make_ops(cnt):
    ops = []
    A, F = AluOpType, ActivationFunctionType

    def add(name, eng, cost, deps, fn, ext=(), bank=None):
        ops.append({"name": name, "eng": eng, "cost": cost, "deps": list(deps), "fn": fn, "ext": list(ext), "bank": bank})

    def move(e, on, out, in_, f=None):
        if on == "V":
            return e.tensor_copy(out, in_) if f is None else e.tensor_scalar(out, in_, f, None, A.mult)
        return e.activation(out, in_, F.Copy) if f is None else e.activation(out, in_, F.Copy, scale=f)

    add("mz", "V", ("h", 644), [], lambda e, T, k, on: e.memset(T.zt[:, 0:644], 0.0))
    add("df", "V", ("c", 128), ["mz"], lambda e, T, k, on: e.tensor_scalar(T.zt[:, 3:515:4], T.ib[:], 0.0, None, A.is_equal), [("G", 1)])
    add("mi", "V", ("h", NT + 16 * NC + 16), ["df"], lambda e, T, k, on: e.tensor_copy(T.mm[:], T.zt[:, 0:NT + 16 * NC + 16]))
    add("ra", "V", ("c", 64), [], lambda e, T, k, on: e.transpose(T.rt[:, 0:64], T.rr[:, 0:64]), [("G", 3)])
    add("de", "F", ("h", 512), ["df", "ra"], lambda e, T, k, on:
        e.tensor_scalar(T.zt[:, 644:1156], T.zt[:, 0:512], T.rt[:, 32:33], 0.0, A.add, A.max) if on == "V" else
        e.activation(T.zt[:, 644:1156], T.zt[:, 0:512], F.Relu, bias=T.rt[:, 32:33]))
    add("do", "F", ("h", 516), ["df", "ra"], lambda e, T, k, on:
        e.tensor_scalar(T.zt[:, 1156:1672], T.zt[:, 0:516], T.rt[:, 32:33], -1.0, A.mult, A.mult) if on == "V" else
        e.activation(T.zt[:, 1156:1672], T.zt[:, 0:516], F.Abs, scale=T.rt[:, 32:33]))
    for b in range(4):
        add("e%d" % b, "V", ("q", 128), ["df"], lambda e, T, k, on, b=b: e.quantize_mx(T.ec[:, 128 * b:128 * b + 128], T.es[:, 128 * b:128 * b + 128], T.zt[:, 3 - b:515 - b]))
        add("f%d" % b, "V", ("q", 256), ["de", "do"], lambda e, T, k, on, b=b:
            e.quantize_mx(T.ec[:, 512 + 256 * b:768 + 256 * b], T.es[:, 512 + 256 * b:768 + 256 * b], T.zt[:, 647 - b:1671 - b]))
    add("wi0", "F", ("c", NP), ["df"], lambda e, T, k, on: move(e, on, T.win0[:], T.zt[:, 0:NP]))
    add("bi", "V", ("c", 1), ["ra"], lambda e, T, k, on: e.tensor_scalar(T.bias[:], T.rt[:, 0:1], 0.5, -2 * TINY, A.subtract, A.mult))
    add("rb", "V", ("c", 64 * len(KINDS)), [], lambda e, T, k, on: e.transpose(T.rt[:, 64:], T.rr[:, 64:]), [("G", 3 + len(list_rows()))])
    for i, n in enumerate(KINDS):
        add("cl%d" % n, "V", ("c", 2), ["rb"], lambda e, T, k, on, i=i, n=n:
            e.tensor_scalar(T.cl[:, 2 * i:2 * i + 2], T.rt[:, 64 + 64 * i:128 + 64 * i:32], float(n // 8 + 1), 0.0, A.min, A.max))
    add("nh", "V", ("c", 80), [], lambda e, T, k, on: e.tensor_scalar(T.nxh[:], T.nxl[:], 0.5, None, A.mult), [("lnx", 16)])
    add("nx0", "V", ("c", 80), ["nh"], lambda e, T, k, on: e.tensor_tensor(T.nxa0[:, 0:40], T.nxh[:, 1:80:2], T.nxh[:, 0:80:2], A.subtract))
    add("nx1", "V", ("c", 80), ["nh"], lambda e, T, k, on: e.tensor_tensor(T.nxa0[:, 40:80], T.nxh[:, 1:80:2], T.nxh[:, 0:80:2], A.add))
    for b in range(4):
        add("s%d" % b, "V", ("c", 28), [], lambda e, T, k, on, b=b: e.tensor_scalar(T.lst0[:, 28 * b:28 * b + 28], T.stw[:], 4.0, float(b), A.mult, A.add), [("lst", 16)])
    add("sn", "V", ("c", 28), [], lambda e, T, k, on: e.tensor_copy(T.lst0[:, 112:140], T.stw[:]), [("lst", 16)])
    add("qa", "V", ("q", HALF), [], lambda e, T, k, on: e.quantize_mx(T.tc0[:, 0:HALF], T.ts0[:, 0:HALF], T.kt[:, 0:4 * HALF]), [("ka", 16)])
    add("qb", "V", ("q", NP - HALF), [], lambda e, T, k, on: e.quantize_mx(T.tc0[:, HALF:NP], T.ts0[:, HALF:NP], T.kt[:, 4 * HALF:4 * NP]), [("kb", 16)])
    add("qu", "V", ("q", 128), [], lambda e, T, k, on: e.quantize_mx(T.tc0[:, NP:TW], T.ts0[:, NP:TW], T.ut[:]), [("lu", 16)])
    add("qv", "V", ("q", 128), [], lambda e, T, k, on: e.quantize_mx(T.qvc[:], T.qvs[:], T.vtile[:]), [("lv", 16)])
    for c in range(NC):
        o, n = span([c])
        add("qs0_%d" % c, "V", ("q", n), [], lambda e, T, k, on, o=o, n=n: e.quantize_mx(T.sc[:, o:o + n], T.ss[:, o:o + n], T.xt[:, 4 * o:4 * (o + n)]), [("x%d" % c, 16)])
    for cs in GSEG:
        o, n = span(cs)
        for b in range(4):
            add("g%d_%d" % (b, cs[0]), "F", ("g", n), ["s%d" % b], lambda e, T, k, on, b=b, o=o, n=n:
                move(e, on, T.nt[:, 4 * o + b:4 * (o + n):4], T.kt[:].indirect(T.lst0[:, 28 * b + o // 16:28 * b + (o + n) // 16])), [("ka", 16), ("kb", 16)])

    for t in range(NH):
        tab = [(s, cnt[s]) for s in ([], ["ka1", "kr1", "kb1"], ["k2"])[t]]
        utab = tab + [(s, cnt[s]) for s in ([], ["u1"], ["u2"])[t]]
        tc, ts, pc, pz, ls = "tc%d" % t, "ts%d" % t, "pc%d" % t, "pz%d" % t, "lst%d" % t
        for c in range(NC):
            o, n = span([c])
            s, nq, nb, h = "%d_%d" % (t, c), n // 16, n // 32, NT * t + o
            if t == 0:
                add("qn%d" % c, "V", ("q", n), ["g%d_%d" % (b, cs[0]) for b in range(4) for cs in GSEG if c in cs], lambda e, T, k, on, o=o, n=n:
                    e.quantize_mx(T.pc0[:, o:o + n], T.pz0[:, o:o + n], T.nt[:, 4 * o:4 * (o + n)]))
                pn, ndep, nat = ["qn%d" % c], ["sn"], 112 + o // 16
            else:
                pn, ndep, nat, l = ["pc" + s, "pz" + s], ["cp%d_%d" % (t - 1, c)], 32 * c + 2 * nq, 32 * c
                add("pc" + s, "V", ("g", 2 * n), ndep, lambda e, T, k, on, o=o, n=n, l=l, tc=tc, pc=pc, ls=ls:
                    e.tensor_copy(T[pc][:, 2 * o:2 * (o + n)].bitcast(dt.uint32), T[tc][:, 0:NP].bitcast(dt.uint32).indirect(T[ls][:, l:l + n // 8])), tab)
                add("pz" + s, "F", ("g", 2 * n), ndep, lambda e, T, k, on, o=o, n=n, l=l, ts=ts, pz=pz, ls=ls:
                    move(e, on, T[pz][:, 2 * o:2 * (o + n)], T[ts][:, 0:NP].indirect(T[ls][:, l:l + n // 8])), tab)
            for b in range(4):
                bk = "%d_%s" % (b, s)

                def state(e, T, k, on, b=b, h=h, n=n):
                    return e.matmul_mx(T.ps[:, 512 * k:512 * k + n], T.ec[:, 128 * b:128 * b + 128], T.es[:, 128 * b:128 * b + 128],
                                       T.sc[:, h:h + n], T.ss[:, h:h + n], on, not on)

                def nodes(e, T, k, on, b=b, t=t, o=o, n=n, pc=pc, pz=pz):
                    out = T.ps[:, 512 * k:512 * k + n]
                    if t == 0:
                        return e.matmul_mx(out, T.ec[:, 128 * b:128 * b + 128], T.es[:, 128 * b:128 * b + 128], T.pc0[:, o:o + n], T.pz0[:, o:o + n], on, not on)
                    eb = 512 + 256 * b
                    e.matmul_mx(out, T.ec[:, eb:eb + 128], T.es[:, eb:eb + 128], T[pc][:, 2 * o:2 * o + n], T[pz][:, 2 * o:2 * o + n], on, False)
                    return e.matmul_mx(out, T.ec[:, eb + 128:eb + 256], T.es[:, eb + 128:eb + 256], T[pc][:, 2 * o + n:2 * o + 2 * n], T[pz][:, 2 * o + n:2 * o + 2 * n], False, not on)
                add("a" + bk, "P", ("p1", n), ["qs" + s, "e%d" % b], state, bank="b" + bk)
                add("n" + bk, "P", ("p2" if t else "p1", n), pn + ["f%d" % b if t else "e%d" % b], nodes, bank="b" + bk)
                add("cv" + bk, "F", ("c", n), ["a" + bk, "n" + bk], lambda e, T, k, on, b=b, t=t, o=o, n=n:
                    move(e, on, T["bt%d" % t][:, 4 * o + b:4 * (o + n):4], T.ps[:, 512 * k:512 * k + n], 0.5), bank="b" + bk)
            add("qv" + s, "V", ("q", n), ["cv%d_%s" % (b, s) for b in range(4)], lambda e, T, k, on, t=t, o=o, n=n, h=h:
                e.quantize_mx(T.vc[:, h:h + n], T.vs[:, h:h + n], T["bt%d" % t][:, 4 * o:4 * (o + n)]))
            for b in range(4):
                bk = "%d_%s" % (b, s)
                add("l" + bk, "P", ("p1", n), ["qv" + s], lambda e, T, k, on, b=b, h=h, n=n:
                    e.matmul_mx(T.ps[:, 512 * k:512 * k + n], T.wqc[:, 128 * b:128 * b + 128], T.wqs[:, 128 * b:128 * b + 128], T.vc[:, h:h + n], T.vs[:, h:h + n], True, True),
                    [("lw", 32)], "l" + bk)
                add("cr" + bk, "F", ("c", n), ["l" + bk], lambda e, T, k, on, b=b, h=h, n=n:
                    move(e, on, T.lt[:, 4 * h + b:4 * (h + n):4], T.ps[:, 512 * k:512 * k + n], 0.03125), bank="l" + bk)
            add("qs%d_%d" % (t + 1, c), "V", ("q", n), ["cr%d_%s" % (b, s) for b in range(4)], lambda e, T, k, on, h=h, n=n:
                e.quantize_mx(T.sc[:, NT + h:NT + h + n], T.ss[:, NT + h:NT + h + n], T.lt[:, 4 * h:4 * (h + n)]))
            add("sc" + s, "P", ("p1", n), ["qv" + s] + (["qu"] if t == 0 else []), lambda e, T, k, on, h=h, n=n, tc=tc, ts=ts:
                e.matmul_mx(T.ps[:, 512 * k:512 * k + n], T[tc][:, NP:TW], T[ts][:, NP:TW], T.vc[:, h:h + n], T.vs[:, h:h + n], True, True), utab, "s" + s)
            add("sg" + s, "S", ("c", n), ["sc" + s, "bi"], lambda e, T, k, on, t=t, o=o, n=n:
                e.activation(T["sg%d" % t][:, o:o + n], T.ps[:, 512 * k:512 * k + n], F.Sign, bias=T.bias[:, 0:1], scale=T.rt[:, 0:1]), bank="s" + s)
            mm, m = ("mm", o + 16 * (c + 1)) if t < NH - 1 else ("ml", o)
            add("mg" + s, "V", ("g", n), ["sg" + s, "mi"] + ndep, lambda e, T, k, on, t=t, o=o, n=n, mm=mm, m=m, ls=ls, nat=nat, nq=nq:
                e.tensor_tensor(T[mm][:, m:m + n], T["win%d" % (t % 2)][:].indirect(T[ls][:, nat:nat + nq]), T["sg%d" % t][:, o:o + n], A.mult), [("w%d" % t, 32)])
            if t == NH - 1:
                add("t1" + s, "V", ("h", n), ["mg" + s], lambda e, T, k, on, o=o, n=n: e.transpose(T.tl[:, o:o + n], T.ml[:, o:o + n]))
                continue
            z, to, lc = 40 * (NC * t + c), 2 * o + 32 * c, 2 * KINDS.index(n)
            add("t1" + s, "V", ("h", n), ["mg" + s], lambda e, T, k, on, n=n, m=m, to=to: e.transpose(T.tt[:, to:to + n], T.mm[:, m:m + n]))
            add("t2" + s, "V", ("h", n + 32), ["mg" + s], lambda e, T, k, on, n=n, m=m, to=to: e.transpose(T.tt[:, to + n:to + 2 * n + 32], T.mm[:, m - 16:m + n + 16]))
            add("mx" + s, "V", ("c", 8 * nb + 4), ["t1" + s, "t2" + s], lambda e, T, k, on, n=n, to=to, z=z, nb=nb:
                e.tensor_tensor(T.zc[:, z:z + 4 * nb + 2], T.tt[:, to:to + 2 * n + 32:16], T.tt[:, to + 1:to + 2 * n + 32:16], A.add))
            add("cp" + s, "V", ("g", 32), ["mx" + s, "cl%d" % n], lambda e, T, k, on, t=t, c=c, z=z, nb=nb, lc=lc:
                e.tensor_copy(T["lst%d" % (t + 1)][:, 32 * c:32 * c + 32], T.zc[:, z:z + 4 * nb + 2].indirect(T.cl[:, lc:lc + 2])))
    for i, cs in enumerate(YSEG):
        o, n = span(cs)
        add("y%d" % i, "P", ("p1", n), ["qs3_%d" % c for c in cs] + ["qv"], lambda e, T, k, on, h=NH * NT + o, n=n:
            e.matmul_mx(T.ps[:, 512 * k:512 * k + n], T.qvc[:], T.qvs[:], T.sc[:, h:h + n], T.ss[:, h:h + n], True, True), bank="y%d" % i)
        add("cy%d" % i, "F", ("c", n), ["y%d" % i], lambda e, T, k, on, o=o, n=n: move(e, on, T.ysb[:, o:o + n], T.ps[:, 512 * k:512 * k + n]), bank="y%d" % i)
    tl = ["t1%d_%d" % (NH - 1, c) for c in range(NC)] + ["nx0", "nx1"]
    for h in range(2):
        add("fm%d" % h, "V", ("c", 28), tl, lambda e, T, k, on, h=h: e.tensor_tensor(T.nxh[:, 14 * h:14 * h + 14], T.tl[:, 16 * h:NT:32], T.tl[:, 16 * h + 1:NT:32], A.add))
    add("ft", "V", ("c", 32), ["fm0", "fm1"], lambda e, T, k, on: e.transpose(T.zo[:], T.nxh[:, 0:32]))
    return ops


def plan(T, topo):
    cores, n = list(T.cores), len(T.cores)
    calls, got = {}, {}

    def call(src, need, *transfers):
        calls.setdefault(src, []).append((need, transfers))
        for dst, a, b, c0, c1, s, eng in transfers:
            got[(dst, s)] = got.get((dst, s), 0) + len(eng)
            got[(src, "sent")] = got.get((src, "sent"), 0) + len(eng)

    for r in range(n):
        me, d1, d2, up = cores[r], cores[(r - 1) % n], cores[(r - 2) % n], cores[(r + 1) % n]
        off = topo.engines(me, d2)
        every = topo.engines(me, [c for c in topo.cores_of(me) if c != me][0])
        rest = [e for e in every if e not in off]
        kids, q = ["nx0", "nx1"], len(off) // 2
        if topo.chip(d1) == topo.chip(me):
            call(me, kids, (d1, "nxa0", "nxa1", 0, 80, "n1", rest), (d2, "nxa0", "nxa2", 0, 80, "n2", off))
            call(me, ["qa", "qb", "qu"], (d1, "tc0", "tc1", 0, TW, "ka1", every))
            call(me, [], (d1, "ts0", "ts1", 0, TW, "kb1", every))
            call(me, ["hr"], (d2, "tch", "tc1", REL, HALF, "kr1", off))
            call(me, [], (d2, "tc0", "tc2", 0, HALF, "k2", off))
            call(me, ["fill", "ka1", "kr1", "kb1"], (d1, "tc1", "tc2", 0, NP, "k2", rest))
            call(me, [], (d1, "ts1", "ts2", 0, TW, "k2", rest), (d2, "ts0", "ts2", 0, TW, "k2", off))
            call(me, ["u1"], (d1, "tc1", "tc2", NP, TW, "u2", rest))
        else:
            call(me, kids, (d1, "nxa0", "nxa1", 0, 80, "n1", off))
            call(me, ["qa"], (d1, "tc0", "tc1", 0, REL, "ka1", off), (up, "tc0", "tch", REL, HALF, "hr", rest))
            call(me, ["qb", "qu"], (d1, "tc0", "tc1", HALF, NP, "kb1", off[:q]), (d1, "ts0", "ts1", 0, TW, "kb1", off[q:]))
            call(me, [], (d1, "tc0", "tc1", NP, TW, "u1", off))
            call(me, [], (d2, "nxa0", "nxa2", 0, 80, "n2", off))
            call(me, ["fill", "ka1"], (d1, "tc1", "tc2", HALF, TW, "k2", off))
    return calls, got


def list_rows():
    rows = []
    for i, n in enumerate(KINDS):
        nb, nq = n // 32, n // 16
        for h in range(2):
            step, base, e = (-2 * nb, 2 * nb, 0) if h else (2 * nb + 2, 0, 0)
            if 2 * nq == 16:
                rows.append((64 + 64 * i + 16 * h, [[1, 2], [2, nq // 2], [step, 2]], base))
                e = 16
            while e < 32:
                l = min(e // nq, 2)
                end = min(e // 16 * 16 + 16, (l + 1) * nq if l < 2 else 32)
                rows.append((64 + 64 * i + 32 * (e // 16) + 16 * h + e % 16, [[2, (end - e) // 2], [step, 2]], base + e - l * nq + (0, 1, h)[l]))
                e = end
    return rows


def lay_out(ops, seq):
    by = {o["name"]: o for o in ops}
    order, bank, before, opens = {"P": [], "V": [], "S": []}, {}, {}, {}
    free = [(k, None) for k in range(8)]
    for x in seq:
        n = x.rstrip("*")
        o = by[n]
        order[o["eng"] if o["eng"] != "F" else "V" if x != n else "S"].append(n)
        r = o["bank"]
        if r and o["eng"] == "P":
            opens[n] = r not in bank
            if opens[n]:
                bank[r], last = free.pop(0)
                if last:
                    before[n] = last
        elif r:
            free.append((bank[r], n))
    return order, bank, before, opens


def waits(order, idx, by, before):
    know, seen, out = {e: {} for e in order}, {}, {}
    pos = {e: 0 for e in order}
    while len(out) < len(idx):
        for e in order:
            while pos[e] < len(order[e]):
                n = order[e][pos[e]]
                ds = by[n]["deps"] + ([before[n]] if n in before else [])
                if any(d not in out for d in ds):
                    break
                want = {}
                for d in ds:
                    want[idx[d][0]] = max(want.get(idx[d][0], 0), idx[d][1])
                for s, v in by[n]["ext"]:
                    want[s] = max(want.get(s, 0), v)
                want = {s: v for s, v in want.items() if know[e].get(s, 0) < v}
                for s in list(want):
                    if any(o != s and o in order and seen[(o, want[o])].get(s, 0) >= want[s] for o in want):
                        del want[s]
                for s, v in want.items():
                    for s2, v2 in list(seen.get((s, v), {}).items()) + [(s, v)]:
                        know[e][s2] = max(know[e].get(s2, 0), v2)
                out[n] = want
                seen[idx[n]] = dict(know[e])
                pos[e] += 1
    return out


def rank_program(g, core, T, topo):
    if T.rank_of(core) is None:
        return
    calls, got = plan(T, topo)
    sem = T.sem
    ops = make_ops({s: got.get((core, s), 0) for s in SEMAPHORES})
    by = {o["name"]: o for o in ops}
    order, bank, before, opens = lay_out(ops, ORDER.split())
    idx = {n: (e, i + 1) for e in order for i, n in enumerate(order[e])}
    todo = waits(order, idx, by, before)

    def waiter(q):
        seen = {}

        def need(s, v):
            if seen.get(s, 0) < v:
                q.wait_ge(sem[s], v)
                seen[s] = v
        return need

    def after(need, ds):
        for e in order:
            need(e, max([0] + [idx[d][1] for d in ds if idx[d][0] == e]))

    sy, sc = g.sync, g.scalar
    sc.dma_start(T.nxl[:], T.nx[:]).then_inc(sem.lnx, 16)
    sc.dma_start(T.stw[:], T.st[:]).then_inc(sem.lst, 16)
    ns = waiter(sy)
    loads = {"ka": [(T.kt[:, 0:4 * HALF], T.k[:, 0:4 * HALF], "ka")], "kb": [(T.kt[:, 4 * HALF:4 * NP], T.k[:, 4 * HALF:4 * NP], "kb")],
             "u": [(T.ut[:], T.u[:], "lu")], "v": [(T.vtile[:], T.v[:], "lv")],
             "W": [(T.wqc[:].bitcast(dt.uint8), T.wc[:], "lw"), (T.wqs[:], T.ws[:], "lw")]}
    for c in range(NC):
        o, n = span([c])
        loads["x%d" % c] = [(T.xt[:, 4 * o:4 * (o + n)], T.x[:, 4 * o:4 * (o + n)], "x%d" % c)]
    for t in range(NH):
        loads["w%d" % t] = [(T["win%d" % (t % 2)][b:128:16, :], T["nxa%d" % t][:, 40 * b:40 * b + 40], "w%d" % t) for b in range(2)]
    for x in LOADS.split():
        if x in ("w0", "w1", "w2"):
            after(ns, {"w0": ["wi0", "nx0", "nx1"], "w1": [], "w2": ["mg0_%d" % c for c in range(NC)]}[x])
            if x != "w0":
                ns("G", 4 + len(list_rows()))
                ns("n" + x[1], got[(core, "n" + x[1])])
        for dst, src, s in loads[x]:
            sy.dma_start(dst, src).then_inc(sem[s], 16)

    stores, last = {}, NH * NT
    for i, cs in enumerate(YSEG):
        o, n = span(cs)
        stores["oc%d" % i] = (["qs3_%d" % c for c in cs], T.oc[:, 4 * o:4 * (o + n)], T.sc[:, last + o:last + o + n].bitcast(dt.uint8))
        stores["y%d" % i] = (["cy%d" % i], T.y[:, o:o + n], T.ysb[:, o:o + n])
    for a in range(4):
        stores["os%d" % a] = (["qs3_%d" % c for c in range(NC)], T.osc[4 * a:4 * a + 4, :], T.ss[32 * a:32 * a + 4, last:last + NT])
        stores["pl%d" % a] = (["ft"], T.pl[2 * a:2 * a + 2, :], T.zo[32 * a:32 * a + 28, :])

    def store(q, need, names):
        for x in names.split():
            ds, dst, src = stores[x]
            after(need, ds)
            q.dma_start(dst, src).then_inc(sem.out, 16)

    for e, q in (("P", g.tensor), ("V", g.vector), ("S", g.scalar)):
        for n in order[e]:
            for s, v in todo[n].items():
                q.wait_ge(sem[s], v)
            by[n]["fn"](q, T, bank.get(by[n]["bank"]), opens[n] if e == "P" else e).then_inc(sem[e], 1)
        if e == "S":
            store(q, waiter(q), STORES[1])
    store(sy, ns, STORES[0])
    for e in order:
        ns(e, len(order[e]))
    ns("out", 16 * len(stores))

    def iota(out, pat, base, mult=0):
        g.iota(out, pat, base, mult, allow_small_or_imprecise_dtypes=True).then_inc(sem.G, 1)

    iota(T.ib[:], [[-1, 128]], 0, 1)
    iota(T.rr[:, 0:32], [[0, 2], [-1, 16]], 1)
    iota(T.rr[:, 32:64], [[-1, 2], [0, 16]], 0)
    for a, pat, base in list_rows():
        iota(T.rr[:, a:a + math.prod(c for s, c in pat)], pat, base)

    ng = waiter(g)
    for need, transfers in calls[core]:
        for d in need:
            if d == "fill":
                iota(T.win1[:], [[0, NP]], 0)
            else:
                ng(*idx.get(d, (d, got.get((core, d), 0))))
        tr = []
        for d, a, b, c0, c1, s, eng in transfers:
            rid, pid, se = topo.addr(d)
            src, dst = T[a][:, c0:c1], T[b][:, c0:c1]
            if a[:2] == "tc":
                src, dst = src.bitcast(dt.uint8), dst.bitcast(dt.uint8)
            tr.append(RemoteDMATransfer(dst_ids=[DstId(rid=rid, pnc=pid)], dma_engine_mask=sum(1 << e for e in eng), remote_sem=sem[s], src=src, dst=dst))
        g.remote_dma_fused(tr, local_sem=sem.sent)
    ng("sent", got[(core, "sent")])
